import numpy as np
import ml_dtypes


def mxq(x, axis, fmt="e4m3"):
    dtype, down = {"e4m3": (ml_dtypes.float8_e4m3fn, 7), "e5m2": (ml_dtypes.float8_e5m2, 14)}[fmt]
    v = np.moveaxis(np.asarray(x, np.float32).astype(ml_dtypes.bfloat16).astype(np.float64), axis, -1)
    blocks = v.reshape(v.shape[:-1] + (-1, 32))
    amax = np.abs(blocks).max(-1, keepdims=True)
    byte = np.maximum(np.where(amax > 0, np.frexp(amax)[1] - 1 + 127, 0) - down, 1)
    scale = np.exp2(byte - 127.0)
    codes = (blocks / scale).astype(np.float32).astype(dtype).astype(np.float64)
    return np.moveaxis((codes * scale).reshape(v.shape), -1, axis)


WIDE = False


def mx_kscale(k):
    if not WIDE:
        return np.ones(k)
    levels = np.array([10, -10, 5, -5, 0])
    if k % 512:
        return np.exp2(np.random.permutation(np.resize(levels, k // 32))).repeat(32)
    a = np.empty((k // 512, 16))
    for p in range(k // 512):
        a[p, :8] = np.random.permutation(np.resize(levels, 8))
        for g in range(8):
            far = levels[np.abs(levels - a[p, g]) >= 10]
            a[p, g + 8] = far[np.random.randint(len(far))]
    return np.exp2(a.ravel()).repeat(32)


def f64(x):
    return np.asarray(x).astype(np.float64)


def striped8(idx):
    return np.concatenate([v.reshape(-1, 16).T for v in idx]).astype(np.uint16)


def unstriped8(offs):
    return np.stack([offs[16 * g:16 * g + 16].T.reshape(-1) for g in range(8)]).astype(np.int64)


E2M1 = np.array([0.0, 0.5, 1.0, 1.5, 2.0, 3.0, 4.0, 6.0, -0.0, -0.5, -1.0, -1.5, -2.0, -3.0, -4.0, -6.0])


def pack_weight(w, fmt):
    k, n = w.shape
    w = f64(np.asarray(w, np.float32).astype(ml_dtypes.bfloat16)).reshape(k // 32, 32, n)
    amax = np.abs(w).max(1)
    if fmt == "e4m3":
        byte = np.frexp(amax)[1] - 1 + 127 - 7
    else:
        mant, ex = np.frexp(amax / 6.0)
        byte = np.where(mant > 0.5, ex, ex - 1) + 127
    byte = np.clip(np.where(amax > 0, byte, 1), 1, 254)
    scaled = (w * np.exp2(127.0 - byte)[:, None, :]).reshape(k, n).astype(np.float32)
    by_word = np.ascontiguousarray(scaled.reshape(k // 512, 128, 4, n).transpose(0, 1, 3, 2))
    if fmt == "e4m3":
        words = by_word.astype(ml_dtypes.float8_e4m3fn).view(np.uint8)
    else:
        c = by_word.astype(ml_dtypes.float4_e2m1fn).view(np.uint8) & 0xF
        words = (c[..., 0::2] | (c[..., 1::2] << 4)).reshape(k // 512, 128, 2 * n)
    return np.ascontiguousarray(words), np.ascontiguousarray(byte.astype(np.uint8).reshape(k // 512, 16, n))


def unpack_weight(words, scales, fmt):
    g, _, n = scales.shape
    words = np.ascontiguousarray(words).reshape(g, 128, n, -1)
    if fmt == "e4m3":
        vals = words.view(ml_dtypes.float8_e4m3fn).astype(np.float64)
    else:
        nib = np.empty((g, 128, n, 4), np.uint8)
        nib[..., 0::2] = words & 0xF
        nib[..., 1::2] = words >> 4
        vals = E2M1[nib]
    vals = vals * np.repeat(np.exp2(scales.astype(np.float64) - 127.0), 8, axis=1)[..., None]
    return vals.transpose(0, 1, 3, 2).reshape(g * 512, n)


K, M, T, S = 1536, 1024, 1024, 512


def setup_inputs():
    n = np.random.standard_normal
    s = mx_kscale(K)[:, None]
    p_w = pack_weight(n((K, M)) / np.sqrt(K) / s, "e2m1")
    return {
        "xT": (n((K, T)) * s).astype(np.float32),
        "w_words": p_w[0],
        "w_scales": p_w[1],
        "wgt": np.repeat(np.random.uniform(0.5, 2.0, (8, S)), 16, axis=0).astype(np.float32),
        "b": (0.3 * n(1024)).astype(np.float32),
        "wgo": np.repeat(np.random.uniform(0.5, 2.0, (8, S)), 16, axis=0).astype(np.float32),
        "offs": striped8(np.stack([np.random.permutation(T)[:S] for _ in range(8)])),
        "offs2": striped8(np.stack([np.random.permutation(T)[:S] for _ in range(8)])),
    }


def reference(xT, w_words, w_scales, wgt, b, wgo, offs, offs2):
    idx = unstriped8(offs)
    group = np.arange(K) % 512 // 64
    xg = f64(wgt)[np.arange(K) // 4 % 128] * f64(xT)[np.arange(K)[:, None], idx[group]]
    xT_ = mxq(xg, 0, "e4m3")
    w_ = unpack_weight(w_words, w_scales, "e2m1")
    y = w_.T @ xT_
    place = unstriped8(offs2)[np.arange(M) % 128 // 16]
    out = np.zeros((M, T))
    out[np.arange(M)[:, None], place] = f64(wgo)[np.arange(M) % 128] * (y + f64(b)[:, None])
    return out

@@ -1,0 +1,193 @@
+import concourse.mybir as mybir
+from concourse.masks import make_identity
+
+K, M, T, S = 1536, 1024, 1024, 512
+
+FLOPS = 2 * K * M * S
+
+F32 = mybir.dt.float32
+BF16 = mybir.dt.bfloat16
+I32 = mybir.dt.int32
+U32 = mybir.dt.uint32
+U16 = mybir.dt.uint16
+U8 = mybir.dt.uint8
+E4M3X4 = mybir.dt.float8_e4m3fn_x4
+E2M1X4 = mybir.dt.float4_e2m1fn_x4
+MULT = mybir.AluOpType.mult
+IDENTITY = mybir.ActivationFunctionType.Identity
+
+P = 128
+PACK = 4
+PASSES = K // (P * PACK)
+M_TILES = M // P
+HALF = S // 2
+HALF_LIST = HALF // 16
+GROUP_N = 128
+VECTOR_ZEROED = 3
+EARLY_TILES = 2
+
+
+def tile_list_hboth_bias_kernel(tc, xT, w_words, w_scales, wgt, b, wgo, offs, offs2, out):
+    nc = tc.nc
+    with (
+        tc.tile_pool(name="lists", bufs=1) as lists,
+        tc.tile_pool(name="keep", bufs=1) as keep,
+        tc.tile_pool(name="work", bufs=2) as work,
+        tc.psum_pool(name="psum", bufs=1) as psum,
+    ):
+        gather_list = lists.tile([P, S // 16], U16, name="gather_list")
+        scatter_list = lists.tile([P, S // 16], U16, name="scatter_list")
+
+        weight = [keep.tile([P, HALF], F32, name=f"weight{h}") for h in range(2)]
+        planes = [keep.tile([P, T], F32, name=f"plane{n}") for n in range(PASSES * PACK)]
+        early_words = keep.tile([P, PASSES, 2 * P * EARLY_TILES], U8, name="early_words", align_bytes=64)
+        late_words = keep.tile([P, PASSES, 2 * P * (M_TILES - EARLY_TILES)], U8, name="late_words", align_bytes=64)
+        scales = keep.tile([P, PASSES, M], U8, name="scales", align_bytes=64)
+        factor = keep.tile([P, S], F32, name="factor")
+        windows = [keep.tile([P, T], F32, name=f"window{m}") for m in range(M_TILES)]
+        bias_rows = keep.tile([P, P], F32, name="bias_rows")
+        identity = keep.tile([P, P], F32, name="identity")
+        bias = keep.tile([P, M_TILES], F32, name="bias")
+        codes = [keep.tile([P, S], U32, name=f"codes{a}", align_bytes=64) for a in range(PASSES)]
+        code_scales = [keep.tile([P, S], U8, name=f"code_scales{a}", align_bytes=64) for a in range(PASSES)]
+
+        nc.sync.dma_start(gather_list[:], offs)
+        for h in range(2):
+            nc.scalar.dma_start(weight[h][:], wgt[:, h * HALF : (h + 1) * HALF])
+        x_view = xT.rearrange("(a p i) t -> a i p t", p=P, i=PACK)
+        for a in range(PASSES):
+            for i in range(PACK):
+                nc.sync.dma_start(planes[a * PACK + i][:], x_view[a, i])
+        nc.vector.memset(scales[:].rearrange("p a n -> p (a n)").bitcast(I32), 0)
+        scales_view = w_scales.bitcast(I32)
+        for q in range(4):
+            nc.sync.dma_start(
+                scales[32 * q : 32 * q + 4, :, :].bitcast(I32),
+                scales_view[:, 4 * q : 4 * q + 4, :].rearrange("a r n -> r a n"),
+            )
+        words_view = w_words.bitcast(I32).rearrange("a p n -> p a n")
+        nc.sync.dma_start(early_words[:].bitcast(I32), words_view[:, :, 0 : EARLY_TILES * P // 2])
+        nc.sync.dma_start(scatter_list[:], offs2)
+        nc.sync.dma_start(factor[:], wgo)
+        nc.sync.dma_start(late_words[:].bitcast(I32), words_view[:, :, EARLY_TILES * P // 2 : M // 2])
+
+        for m in range(VECTOR_ZEROED):
+            nc.vector.memset(windows[m][:].bitcast(I32), 0)
+
+        nc.gpsimd.memset(bias_rows[:], 0.0)
+        nc.gpsimd.dma_start(bias_rows[0:M_TILES, :], b.rearrange("(m p) -> m p", p=P))
+        make_identity(nc, identity[:])
+        for m in range(VECTOR_ZEROED, M_TILES):
+            nc.gpsimd.memset(windows[m][:].bitcast(I32), 0)
+
+        banks = [psum.tile([P, S], F32, name=f"bank{m}") for m in range(M_TILES)]
+        nc.tensor.transpose(banks[M_TILES - 1][:, 0:P], bias_rows[:], identity[:])
+        nc.scalar.copy(bias[:], banks[M_TILES - 1][:, 0:M_TILES])
+
+        def gather(a, i, h, picked):
+            nc.vector.tensor_tensor(
+                picked[:, i, :],
+                planes[a * PACK + i][:].indirect(gather_list[:, h * HALF_LIST : (h + 1) * HALF_LIST]),
+                weight[h][:],
+                MULT,
+            )
+
+        def interleave(picked, grouped, h):
+            nc.scalar.copy(
+                grouped[:, h * HALF : (h + 1) * HALF, :].rearrange("p (c j) i -> p c i j", j=4),
+                picked[:].rearrange("p i (c j) -> p c i j", j=4),
+            )
+
+        def quantize(a, grouped, c0, c1):
+            nc.vector.quantize_mx(
+                out=codes[a][:, c0:c1].bitcast(E4M3X4),
+                scales=code_scales[a][:, c0:c1],
+                in_=grouped[:, c0:c1, :].rearrange("p c i -> p (c i)"),
+            )
+
+        waiting = None
+        for a in range(PASSES - 1):
+            picked = [work.tile([P, PACK, HALF], F32, name=f"picked{h}") for h in range(2)]
+            grouped = work.tile([P, S, PACK], BF16, name="grouped", align_bytes=64)
+            for i in range(PACK):
+                for h in range(2):
+                    gather(a, i, h, picked[h])
+                if i == 2 and waiting is not None:
+                    quantize(a - 1, waiting, 0, S)
+            for h in range(2):
+                interleave(picked[h], grouped, h)
+            waiting = grouped
+
+        last = PASSES - 1
+        picked = [work.tile([P, PACK, HALF], F32, name=f"picked{h}") for h in range(2)]
+        grouped = work.tile([P, S, PACK], BF16, name="grouped", align_bytes=64)
+        for i in range(PACK - 1):
+            for h in range(2):
+                gather(last, i, h, picked[h])
+            if i == 1:
+                quantize(last - 1, waiting, 0, S)
+        for c0 in range(0, HALF, GROUP_N):
+            nc.vector.tensor_tensor(
+                picked[0][:, PACK - 1, c0 : c0 + GROUP_N],
+                planes[-1][:].indirect(gather_list[:, c0 // 16 : (c0 + GROUP_N) // 16]),
+                weight[0][:, c0 : c0 + GROUP_N],
+                MULT,
+            )
+        for c0, copy in ((0, nc.scalar.copy), (GROUP_N, nc.vector.tensor_copy)):
+            copy(
+                grouped[:, c0 : c0 + GROUP_N, :].rearrange("p (c j) i -> p c i j", j=4),
+                picked[0][:, :, c0 : c0 + GROUP_N].rearrange("p i (c j) -> p c i j", j=4),
+            )
+        quantize(last, grouped, 0, HALF)
+        gather(last, PACK - 1, 1, picked[1])
+
+        sums = [[keep.tile([P, HALF], F32, name=f"sum{h}_{m}") for m in range(M_TILES)] for h in range(2)]
+
+        def product(m, h, c):
+            slot = 2 * m + c
+            return banks[slot % M_TILES][:, h * HALF + GROUP_N * (slot // M_TILES) : h * HALF + GROUP_N * (slot // M_TILES + 1)]
+
+        def multiply(m, h, c, passes):
+            c0 = h * HALF + c * GROUP_N
+            for a in passes:
+                if m < EARLY_TILES:
+                    lhsT = early_words[:, a, 2 * P * m : 2 * P * (m + 1)]
+                else:
+                    lhsT = late_words[:, a, 2 * P * (m - EARLY_TILES) : 2 * P * (m - EARLY_TILES + 1)]
+                nc.tensor.matmul_mx(
+                    out=product(m, h, c),
+                    lhsT=lhsT.bitcast(E2M1X4),
+                    lhsT_scale=scales[:, a, P * m : P * (m + 1)],
+                    rhs=codes[a][:, c0 : c0 + GROUP_N].bitcast(E4M3X4),
+                    rhs_scale=code_scales[a][:, c0 : c0 + GROUP_N],
+                    start=(a == 0),
+                    stop=(a == PASSES - 1),
+                )
+
+        def add_bias(m, h, c):
+            nc.scalar.activation(
+                sums[h][m][:, c * GROUP_N : (c + 1) * GROUP_N], product(m, h, c), IDENTITY, bias=bias[:, m : m + 1]
+            )
+
+        def scatter(m, h):
+            nc.vector.tensor_tensor(
+                windows[m][:].indirect(scatter_list[:, h * HALF_LIST : (h + 1) * HALF_LIST]),
+                sums[h][m][:],
+                factor[:, h * HALF : (h + 1) * HALF],
+                MULT,
+            )
+
+        for c in range(2):
+            multiply(0, 0, c, range(PASSES - 1))
+        for h in range(2):
+            for m in range(M_TILES):
+                for c in range(2):
+                    multiply(m, h, c, range(PASSES - 1, PASSES) if h == m == 0 else range(PASSES))
+                    add_bias(m, h, c)
+                scatter(m, h)
+                if h == 0 and m == 1:
+                    interleave(picked[1], grouped, 1)
+                if h == 0 and m == 2:
+                    quantize(last, grouped, HALF, S)
+                if h == 1:
+                    nc.sync.dma_start(out[P * m : P * (m + 1), :], windows[m][:])

@@ -21,10 +21,9 @@ PACK = 4
 PASSES = K // (P * PACK)
 M_TILES = M // P
 HALF = S // 2
-HALF_LIST = HALF // 16
 GROUP_N = 128
-VECTOR_ZEROED = 3
-EARLY_TILES = 2
+SPLIT_TILES = 2
+WINDOWS = 3
 
 
 def tile_list_hboth_bias_kernel(tc, xT, w_words, w_scales, wgt, b, wgo, offs, offs2, out):
@@ -33,31 +32,45 @@ def tile_list_hboth_bias_kernel(tc, xT, w_words, w_scales, wgt, b, wgo, offs, of
         tc.tile_pool(name="lists", bufs=1) as lists,
         tc.tile_pool(name="keep", bufs=1) as keep,
         tc.tile_pool(name="work", bufs=2) as work,
-        tc.psum_pool(name="psum", bufs=1) as psum,
+        tc.psum_pool(name="split_psum", bufs=1) as split_psum,
+        tc.psum_pool(name="whole_psum", bufs=2) as whole_psum,
     ):
         gather_list = lists.tile([P, S // 16], U16, name="gather_list")
         scatter_list = lists.tile([P, S // 16], U16, name="scatter_list")
 
-        weight = [keep.tile([P, HALF], F32, name=f"weight{h}") for h in range(2)]
+        weight = keep.tile([P, S], F32, name="weight")
         planes = [keep.tile([P, T], F32, name=f"plane{n}") for n in range(PASSES * PACK)]
-        early_words = keep.tile([P, PASSES, 2 * P * EARLY_TILES], U8, name="early_words", align_bytes=64)
-        late_words = keep.tile([P, PASSES, 2 * P * (M_TILES - EARLY_TILES)], U8, name="late_words", align_bytes=64)
+        early_words = keep.tile([P, PASSES, 2 * P * SPLIT_TILES], U8, name="early_words", align_bytes=64)
+        late_words = keep.tile([P, PASSES, 2 * P * (M_TILES - SPLIT_TILES)], U8, name="late_words", align_bytes=64)
         scales = keep.tile([P, PASSES, M], U8, name="scales", align_bytes=64)
         factor = keep.tile([P, S], F32, name="factor")
-        windows = [keep.tile([P, T], F32, name=f"window{m}") for m in range(M_TILES)]
+        windows = [keep.tile([P, T], F32, name=f"window{n}") for n in range(WINDOWS)]
         bias_rows = keep.tile([P, P], F32, name="bias_rows")
         identity = keep.tile([P, P], F32, name="identity")
         bias = keep.tile([P, M_TILES], F32, name="bias")
-        codes = [keep.tile([P, S], U32, name=f"codes{a}", align_bytes=64) for a in range(PASSES)]
+        chunk_weight = keep.tile([P, GROUP_N], F32, name="chunk_weight", tag="held", align_bytes=64)
+        codes = {a: keep.tile([P, S], U32, name=f"codes{a}", align_bytes=64) for a in (0, 2)}
         code_scales = [keep.tile([P, S], U8, name=f"code_scales{a}", align_bytes=64) for a in range(PASSES)]
+        first_grouped = keep.tile([P, PACK * HALF], BF16, name="first_grouped", align_bytes=64)
+        half_sums = keep.tile([P, 1 + SPLIT_TILES, HALF], F32, name="half_sums")
+        shared = keep.tile([P, (PACK + 2) * HALF], F32, name="shared")
+        second_words = keep.tile([P, 2 * HALF], F32, name="second_words", align_bytes=64)
 
-        nc.sync.dma_start(gather_list[:], offs)
-        for h in range(2):
-            nc.scalar.dma_start(weight[h][:], wgt[:, h * HALF : (h + 1) * HALF])
+        second_picked = shared[:, 0 : PACK * HALF].rearrange("p (i j) -> p i j", i=PACK)
+        last_weight = shared[:, HALF : HALF + GROUP_N]
+        first_picked = shared[:, 2 * HALF : (PACK + 2) * HALF].rearrange("p (i j) -> p i j", i=PACK)
+        second_grouped = second_words[:].bitcast(BF16)
+        first_bias = second_words[:, 0:1]
+
         x_view = xT.rearrange("(a p i) t -> a i p t", p=P, i=PACK)
-        for a in range(PASSES):
-            for i in range(PACK):
-                nc.sync.dma_start(planes[a * PACK + i][:], x_view[a, i])
+        nc.sync.dma_start(gather_list[:], offs)
+        nc.sync.dma_start(planes[0][:], x_view[0, 0])
+        for h in range(2):
+            nc.sync.dma_start(weight[:, h * HALF : (h + 1) * HALF], wgt[:, h * HALF : (h + 1) * HALF])
+        for n in range(1, PASSES * PACK):
+            nc.sync.dma_start(planes[n][:], x_view[n // PACK, n % PACK])
+        for window in windows:
+            nc.vector.memset(window[:].bitcast(I32), 0)
         nc.vector.memset(scales[:].rearrange("p a n -> p (a n)").bitcast(I32), 0)
         scales_view = w_scales.bitcast(I32)
         for q in range(4):
@@ -66,128 +79,110 @@ def tile_list_hboth_bias_kernel(tc, xT, w_words, w_scales, wgt, b, wgo, offs, of
                 scales_view[:, 4 * q : 4 * q + 4, :].rearrange("a r n -> r a n"),
             )
         words_view = w_words.bitcast(I32).rearrange("a p n -> p a n")
-        nc.sync.dma_start(early_words[:].bitcast(I32), words_view[:, :, 0 : EARLY_TILES * P // 2])
+        nc.sync.dma_start(early_words[:].bitcast(I32), words_view[:, :, 0 : SPLIT_TILES * P // 2])
         nc.sync.dma_start(scatter_list[:], offs2)
         nc.sync.dma_start(factor[:], wgo)
-        nc.sync.dma_start(late_words[:].bitcast(I32), words_view[:, :, EARLY_TILES * P // 2 : M // 2])
-
-        for m in range(VECTOR_ZEROED):
-            nc.vector.memset(windows[m][:].bitcast(I32), 0)
+        nc.sync.dma_start(late_words[:].bitcast(I32), words_view[:, :, SPLIT_TILES * P // 2 : M // 2])
 
         nc.gpsimd.memset(bias_rows[:], 0.0)
-        nc.gpsimd.dma_start(bias_rows[0:M_TILES, :], b.rearrange("(m p) -> m p", p=P))
+        nc.scalar.dma_start(bias_rows[0:M_TILES, :], b.rearrange("(m p) -> m p", p=P))
         make_identity(nc, identity[:])
-        for m in range(VECTOR_ZEROED, M_TILES):
-            nc.gpsimd.memset(windows[m][:].bitcast(I32), 0)
 
-        banks = [psum.tile([P, S], F32, name=f"bank{m}") for m in range(M_TILES)]
-        nc.tensor.transpose(banks[M_TILES - 1][:, 0:P], bias_rows[:], identity[:])
-        nc.scalar.copy(bias[:], banks[M_TILES - 1][:, 0:M_TILES])
+        turned = whole_psum.tile([P, S], F32, name="whole_bank")
+        nc.tensor.transpose(turned[:, 0:P], bias_rows[:], identity[:])
+        nc.scalar.copy(bias[:], turned[:, 0:M_TILES])
+        nc.scalar.copy(first_bias, turned[:, 0:1])
+        nc.scalar.copy(chunk_weight[:], weight[:, 0:GROUP_N])
+        nc.scalar.copy(last_weight, weight[:, GROUP_N:HALF])
 
-        def gather(a, i, h, picked):
-            nc.vector.tensor_tensor(
-                picked[:, i, :],
-                planes[a * PACK + i][:].indirect(gather_list[:, h * HALF_LIST : (h + 1) * HALF_LIST]),
-                weight[h][:],
-                MULT,
-            )
+        def gather(picked, n, c0, c1, factors):
+            nc.vector.tensor_tensor(picked, planes[n][:].indirect(gather_list[:, c0 // 16 : c1 // 16]), factors, MULT)
 
-        def interleave(picked, grouped, h):
+        def interleave(grouped, picked):
             nc.scalar.copy(
-                grouped[:, h * HALF : (h + 1) * HALF, :].rearrange("p (c j) i -> p c i j", j=4),
-                picked[:].rearrange("p i (c j) -> p c i j", j=4),
+                grouped.rearrange("p (c j i) -> p c i j", j=4, i=PACK),
+                picked.rearrange("p i (c j) -> p c i j", j=4),
             )
 
         def quantize(a, grouped, c0, c1):
-            nc.vector.quantize_mx(
-                out=codes[a][:, c0:c1].bitcast(E4M3X4),
-                scales=code_scales[a][:, c0:c1],
-                in_=grouped[:, c0:c1, :].rearrange("p c i -> p (c i)"),
-            )
-
-        waiting = None
-        for a in range(PASSES - 1):
-            picked = [work.tile([P, PACK, HALF], F32, name=f"picked{h}") for h in range(2)]
-            grouped = work.tile([P, S, PACK], BF16, name="grouped", align_bytes=64)
-            for i in range(PACK):
-                for h in range(2):
-                    gather(a, i, h, picked[h])
-                if i == 2 and waiting is not None:
-                    quantize(a - 1, waiting, 0, S)
-            for h in range(2):
-                interleave(picked[h], grouped, h)
-            waiting = grouped
+            nc.vector.quantize_mx(out=codes[a][:, c0:c1].bitcast(E4M3X4), scales=code_scales[a][:, c0:c1], in_=grouped)
 
         last = PASSES - 1
-        picked = [work.tile([P, PACK, HALF], F32, name=f"picked{h}") for h in range(2)]
-        grouped = work.tile([P, S, PACK], BF16, name="grouped", align_bytes=64)
+        for a in range(last):
+            picked = work.tile([P, PACK, S], F32, name="picked")
+            grouped = work.tile([P, S * PACK], BF16, name="grouped", align_bytes=64)
+            for i in range(PACK):
+                for c0, c1 in ((0, HALF), (HALF, S)) if a == i == 0 or i == PACK - 1 else ((0, S),):
+                    gather(picked[:, i, c0:c1], a * PACK + i, c0, c1, weight[:, c0:c1])
+            for c0 in (0, HALF):
+                interleave(grouped[:, PACK * c0 : PACK * (c0 + HALF)], picked[:, :, c0 : c0 + HALF])
+            if a == 0:
+                quantize(a, grouped[:], 0, S)
+
         for i in range(PACK - 1):
-            for h in range(2):
-                gather(last, i, h, picked[h])
-            if i == 1:
-                quantize(last - 1, waiting, 0, S)
+            gather(first_picked[:, i, :], last * PACK + i, 0, HALF, weight[:, 0:HALF])
+        gather(first_picked[:, PACK - 1, 0:GROUP_N], len(planes) - 1, 0, GROUP_N, chunk_weight[:])
+        gather(first_picked[:, PACK - 1, GROUP_N:HALF], len(planes) - 1, GROUP_N, HALF, last_weight)
+        codes[1] = keep.tile([P, S], U32, name="codes1", tag="held", align_bytes=64)
+        quantize(1, grouped[:], 0, S)
         for c0 in range(0, HALF, GROUP_N):
+            chunk = first_grouped[:, PACK * c0 : PACK * (c0 + GROUP_N)]
+            interleave(chunk, first_picked[:, :, c0 : c0 + GROUP_N])
+            quantize(last, chunk, c0, c0 + GROUP_N)
+        for i in range(PACK):
+            gather(second_picked[:, i, :], last * PACK + i, HALF, S, weight[:, HALF:S])
+
+        def multiply(product, m, a, c0, c1, start, stop):
+            if m < SPLIT_TILES:
+                lhsT = early_words[:, a, 2 * P * m : 2 * P * (m + 1)]
+            else:
+                lhsT = late_words[:, a, 2 * P * (m - SPLIT_TILES) : 2 * P * (m - SPLIT_TILES + 1)]
+            nc.tensor.matmul_mx(
+                out=product,
+                lhsT=lhsT.bitcast(E2M1X4),
+                lhsT_scale=scales[:, a, P * m : P * (m + 1)],
+                rhs=codes[a][:, c0:c1].bitcast(E4M3X4),
+                rhs_scale=code_scales[a][:, c0:c1],
+                start=start,
+                stop=stop,
+            )
+
+        def scatter(m, sums, c0, c1):
             nc.vector.tensor_tensor(
-                picked[0][:, PACK - 1, c0 : c0 + GROUP_N],
-                planes[-1][:].indirect(gather_list[:, c0 // 16 : (c0 + GROUP_N) // 16]),
-                weight[0][:, c0 : c0 + GROUP_N],
-                MULT,
-            )
-        for c0, copy in ((0, nc.scalar.copy), (GROUP_N, nc.vector.tensor_copy)):
-            copy(
-                grouped[:, c0 : c0 + GROUP_N, :].rearrange("p (c j) i -> p c i j", j=4),
-                picked[0][:, :, c0 : c0 + GROUP_N].rearrange("p i (c j) -> p c i j", j=4),
-            )
-        quantize(last, grouped, 0, HALF)
-        gather(last, PACK - 1, 1, picked[1])
-
-        sums = [[keep.tile([P, HALF], F32, name=f"sum{h}_{m}") for m in range(M_TILES)] for h in range(2)]
-
-        def product(m, h, c):
-            slot = 2 * m + c
-            return banks[slot % M_TILES][:, h * HALF + GROUP_N * (slot // M_TILES) : h * HALF + GROUP_N * (slot // M_TILES + 1)]
-
-        def multiply(m, h, c, passes):
-            c0 = h * HALF + c * GROUP_N
-            for a in passes:
-                if m < EARLY_TILES:
-                    lhsT = early_words[:, a, 2 * P * m : 2 * P * (m + 1)]
-                else:
-                    lhsT = late_words[:, a, 2 * P * (m - EARLY_TILES) : 2 * P * (m - EARLY_TILES + 1)]
-                nc.tensor.matmul_mx(
-                    out=product(m, h, c),
-                    lhsT=lhsT.bitcast(E2M1X4),
-                    lhsT_scale=scales[:, a, P * m : P * (m + 1)],
-                    rhs=codes[a][:, c0 : c0 + GROUP_N].bitcast(E4M3X4),
-                    rhs_scale=code_scales[a][:, c0 : c0 + GROUP_N],
-                    start=(a == 0),
-                    stop=(a == PASSES - 1),
-                )
-
-        def add_bias(m, h, c):
-            nc.scalar.activation(
-                sums[h][m][:, c * GROUP_N : (c + 1) * GROUP_N], product(m, h, c), IDENTITY, bias=bias[:, m : m + 1]
+                windows[m % WINDOWS][:].indirect(scatter_list[:, c0 // 16 : c1 // 16]), sums, factor[:, c0:c1], MULT
             )
 
-        def scatter(m, h):
-            nc.vector.tensor_tensor(
-                windows[m][:].indirect(scatter_list[:, h * HALF_LIST : (h + 1) * HALF_LIST]),
-                sums[h][m][:],
-                factor[:, h * HALF : (h + 1) * HALF],
-                MULT,
-            )
+        def store(m):
+            nc.sync.dma_start(out[P * m : P * (m + 1), :], windows[m % WINDOWS][:])
 
-        for c in range(2):
-            multiply(0, 0, c, range(PASSES - 1))
-        for h in range(2):
-            for m in range(M_TILES):
-                for c in range(2):
-                    multiply(m, h, c, range(PASSES - 1, PASSES) if h == m == 0 else range(PASSES))
-                    add_bias(m, h, c)
-                scatter(m, h)
-                if h == 0 and m == 1:
-                    interleave(picked[1], grouped, 1)
-                if h == 0 and m == 2:
-                    quantize(last, grouped, HALF, S)
-                if h == 1:
-                    nc.sync.dma_start(out[P * m : P * (m + 1), :], windows[m][:])
+        def half_tile(m, h, bias_column, sums):
+            bank = split_psum.tile([P, S], F32, name=f"bank{h}_{m}")
+            for a in range(PASSES):
+                for c in range(0, HALF, GROUP_N):
+                    multiply(
+                        bank[:, c : c + GROUP_N], m, a, h * HALF + c, h * HALF + c + GROUP_N,
+                        start=(a == 0 and c == 0), stop=(a == last and c == HALF - GROUP_N),
+                    )
+            nc.scalar.activation(sums, bank[:, 0:HALF], IDENTITY, bias=bias_column)
+            scatter(m, sums, h * HALF, (h + 1) * HALF)
+
+        for c0 in range(0, HALF, GROUP_N):
+            bank = split_psum.tile([P, S], F32, name=f"first_bank{c0}")
+            for a in range(PASSES):
+                multiply(bank[:, 0:GROUP_N], 0, a, c0, c0 + GROUP_N, start=(a == 0), stop=(a == last))
+            nc.scalar.activation(half_sums[:, 0, c0 : c0 + GROUP_N], bank[:, 0:GROUP_N], IDENTITY, bias=first_bias)
+        scatter(0, half_sums[:, 0, :], 0, HALF)
+        interleave(second_grouped, second_picked)
+        quantize(last, second_grouped, HALF, S)
+        half_tile(1, 0, bias[:, 1:2], shared[:, 0:HALF])
+        for m in range(SPLIT_TILES):
+            half_tile(m, 1, bias[:, m : m + 1], half_sums[:, 1 + m, :])
+            store(m)
+        for m in range(SPLIT_TILES, M_TILES):
+            bank = whole_psum.tile([P, S], F32, name="whole_bank")
+            for a in range(PASSES):
+                multiply(bank[:], m, a, 0, S, start=(a == 0), stop=(a == last))
+            sums = work.tile([P, S], F32, name="sums")
+            nc.scalar.activation(sums[:], bank[:], IDENTITY, bias=bias[:, m : m + 1])
+            scatter(m, sums[:], 0, S)
+            store(m)

@@ -39,12 +39,12 @@ def tile_list_hboth_bias_kernel(tc, xT, w_words, w_scales, wgt, b, wgo, offs, of
         scatter_list = lists.tile([P, S // 16], U16, name="scatter_list")
 
         weight = keep.tile([P, S], F32, name="weight")
-        planes = [keep.tile([P, T], F32, name=f"plane{n}") for n in range(PASSES * PACK)]
+        planes = [keep.tile([P, T], F32, name=f"plane{n}", tag=f"slot{n}") for n in range(PASSES * PACK)]
         early_words = keep.tile([P, PASSES, 2 * P * SPLIT_TILES], U8, name="early_words", align_bytes=64)
         late_words = keep.tile([P, PASSES, 2 * P * (M_TILES - SPLIT_TILES)], U8, name="late_words", align_bytes=64)
         scales = keep.tile([P, PASSES, M], U8, name="scales", align_bytes=64)
         factor = keep.tile([P, S], F32, name="factor")
-        windows = [keep.tile([P, T], F32, name=f"window{n}") for n in range(WINDOWS)]
+        windows = [keep.tile([P, T], F32, name=f"window{n}") for n in range(WINDOWS - 1)]
         bias_rows = keep.tile([P, P], F32, name="bias_rows")
         identity = keep.tile([P, P], F32, name="identity")
         bias = keep.tile([P, M_TILES], F32, name="bias")
@@ -119,6 +119,8 @@ def tile_list_hboth_bias_kernel(tc, xT, w_words, w_scales, wgt, b, wgo, offs, of
             if a == 0:
                 quantize(a, grouped[:], 0, S)
 
+        windows.append(keep.tile([P, T], F32, name="last_window", tag="slot0"))
+        nc.gpsimd.memset(windows[-1][:].bitcast(I32), 0)
         for i in range(PACK - 1):
             gather(first_picked[:, i, :], last * PACK + i, 0, HALF, weight[:, 0:HALF])
         gather(first_picked[:, PACK - 1, 0:GROUP_N], len(planes) - 1, 0, GROUP_N, chunk_weight[:])

@@ -22,8 +22,8 @@ PASSES = K // (P * PACK)
 M_TILES = M // P
 HALF = S // 2
 GROUP_N = 128
-SPLIT_TILES = 2
-WINDOWS = 3
+SPLIT_TILES = 3
+WINDOWS = 4
 
 
 def tile_list_hboth_bias_kernel(tc, xT, w_words, w_scales, wgt, b, wgo, offs, offs2, out):
@@ -32,7 +32,6 @@ def tile_list_hboth_bias_kernel(tc, xT, w_words, w_scales, wgt, b, wgo, offs, of
         tc.tile_pool(name="lists", bufs=1) as lists,
         tc.tile_pool(name="keep", bufs=1) as keep,
         tc.tile_pool(name="work", bufs=2) as work,
-        tc.psum_pool(name="split_psum", bufs=1) as split_psum,
         tc.psum_pool(name="whole_psum", bufs=2) as whole_psum,
     ):
         gather_list = lists.tile([P, S // 16], U16, name="gather_list")
@@ -44,7 +43,7 @@ def tile_list_hboth_bias_kernel(tc, xT, w_words, w_scales, wgt, b, wgo, offs, of
         late_words = keep.tile([P, PASSES, 2 * P * (M_TILES - SPLIT_TILES)], U8, name="late_words", align_bytes=64)
         scales = keep.tile([P, PASSES, M], U8, name="scales", align_bytes=64)
         factor = keep.tile([P, S], F32, name="factor")
-        windows = [keep.tile([P, T], F32, name=f"window{n}") for n in range(WINDOWS - 1)]
+        windows = [keep.tile([P, T], F32, name=f"window{n}") for n in range(2)]
         bias_rows = keep.tile([P, P], F32, name="bias_rows")
         identity = keep.tile([P, P], F32, name="identity")
         bias = keep.tile([P, M_TILES], F32, name="bias")
@@ -52,15 +51,16 @@ def tile_list_hboth_bias_kernel(tc, xT, w_words, w_scales, wgt, b, wgo, offs, of
         codes = {a: keep.tile([P, S], U32, name=f"codes{a}", align_bytes=64) for a in (0, 2)}
         code_scales = [keep.tile([P, S], U8, name=f"code_scales{a}", align_bytes=64) for a in range(PASSES)]
         first_grouped = keep.tile([P, PACK * HALF], BF16, name="first_grouped", align_bytes=64)
-        half_sums = keep.tile([P, 1 + SPLIT_TILES, HALF], F32, name="half_sums")
-        shared = keep.tile([P, (PACK + 2) * HALF], F32, name="shared")
+        half_sums = keep.tile([P, 2 + SPLIT_TILES, HALF], F32, name="half_sums")
+        shared = keep.tile([P, PACK * S], F32, name="shared")
         second_words = keep.tile([P, 2 * HALF], F32, name="second_words", align_bytes=64)
 
-        second_picked = shared[:, 0 : PACK * HALF].rearrange("p (i j) -> p i j", i=PACK)
-        last_weight = shared[:, HALF : HALF + GROUP_N]
-        first_picked = shared[:, 2 * HALF : (PACK + 2) * HALF].rearrange("p (i j) -> p i j", i=PACK)
+        last_picked = shared[:].rearrange("p (i j) -> p i j", i=PACK)
+        first_picked = last_picked[:, :, 0:HALF]
+        second_picked = shared[:, HALF : 7 * HALF].rearrange("p (u v j) -> p u v j", u=2, v=3)[:, :, ::2, :]
+        last_weight = second_picked[:, 0, 1, 0:GROUP_N]
         second_grouped = second_words[:].bitcast(BF16)
-        first_bias = second_words[:, 0:1]
+        first_bias = second_words[:, 0:2]
 
         x_view = xT.rearrange("(a p i) t -> a i p t", p=P, i=PACK)
         nc.sync.dma_start(gather_list[:], offs)
@@ -91,7 +91,7 @@ def tile_list_hboth_bias_kernel(tc, xT, w_words, w_scales, wgt, b, wgo, offs, of
         turned = whole_psum.tile([P, S], F32, name="whole_bank")
         nc.tensor.transpose(turned[:, 0:P], bias_rows[:], identity[:])
         nc.scalar.copy(bias[:], turned[:, 0:M_TILES])
-        nc.scalar.copy(first_bias, turned[:, 0:1])
+        nc.scalar.copy(first_bias, turned[:, 0:2])
         nc.scalar.copy(chunk_weight[:], weight[:, 0:GROUP_N])
         nc.scalar.copy(last_weight, weight[:, GROUP_N:HALF])
 
@@ -119,9 +119,11 @@ def tile_list_hboth_bias_kernel(tc, xT, w_words, w_scales, wgt, b, wgo, offs, of
             if a == 0:
                 quantize(a, grouped[:], 0, S)
 
-        windows.append(keep.tile([P, T], F32, name="last_window", tag="slot0"))
-        nc.gpsimd.memset(windows[-1][:].bitcast(I32), 0)
-        for i in range(PACK - 1):
+        for n in range(WINDOWS - 2):
+            windows.append(keep.tile([P, T], F32, name=f"late_window{n}", tag=f"slot{n}"))
+            nc.gpsimd.memset(windows[-1][:].bitcast(I32), 0)
+        gather(last_picked[:, 0, :], last * PACK, 0, S, weight[:])
+        for i in range(1, PACK - 1):
             gather(first_picked[:, i, :], last * PACK + i, 0, HALF, weight[:, 0:HALF])
         gather(first_picked[:, PACK - 1, 0:GROUP_N], len(planes) - 1, 0, GROUP_N, chunk_weight[:])
         gather(first_picked[:, PACK - 1, GROUP_N:HALF], len(planes) - 1, GROUP_N, HALF, last_weight)
@@ -131,8 +133,8 @@ def tile_list_hboth_bias_kernel(tc, xT, w_words, w_scales, wgt, b, wgo, offs, of
             chunk = first_grouped[:, PACK * c0 : PACK * (c0 + GROUP_N)]
             interleave(chunk, first_picked[:, :, c0 : c0 + GROUP_N])
             quantize(last, chunk, c0, c0 + GROUP_N)
-        for i in range(PACK):
-            gather(second_picked[:, i, :], last * PACK + i, HALF, S, weight[:, HALF:S])
+        for i in range(1, PACK):
+            gather(second_picked[:, i // 2, i % 2, :], last * PACK + i, HALF, S, weight[:, HALF:S])
 
         def multiply(product, m, a, c0, c1, start, stop):
             if m < SPLIT_TILES:
@@ -158,7 +160,7 @@ def tile_list_hboth_bias_kernel(tc, xT, w_words, w_scales, wgt, b, wgo, offs, of
             nc.sync.dma_start(out[P * m : P * (m + 1), :], windows[m % WINDOWS][:])
 
         def half_tile(m, h, bias_column, sums):
-            bank = split_psum.tile([P, S], F32, name=f"bank{h}_{m}")
+            bank = whole_psum.tile([P, S], F32, name="whole_bank")
             for a in range(PASSES):
                 for c in range(0, HALF, GROUP_N):
                     multiply(
@@ -169,16 +171,20 @@ def tile_list_hboth_bias_kernel(tc, xT, w_words, w_scales, wgt, b, wgo, offs, of
             scatter(m, sums, h * HALF, (h + 1) * HALF)
 
         for c0 in range(0, HALF, GROUP_N):
-            bank = split_psum.tile([P, S], F32, name=f"first_bank{c0}")
+            bank = whole_psum.tile([P, S], F32, name="whole_bank")
             for a in range(PASSES):
                 multiply(bank[:, 0:GROUP_N], 0, a, c0, c0 + GROUP_N, start=(a == 0), stop=(a == last))
-            nc.scalar.activation(half_sums[:, 0, c0 : c0 + GROUP_N], bank[:, 0:GROUP_N], IDENTITY, bias=first_bias)
+            nc.scalar.activation(half_sums[:, 0, c0 : c0 + GROUP_N], bank[:, 0:GROUP_N], IDENTITY, bias=first_bias[:, 0:1])
         scatter(0, half_sums[:, 0, :], 0, HALF)
-        interleave(second_grouped, second_picked)
+        half_tile(1, 0, first_bias[:, 1:2], half_sums[:, 1, :])
+        nc.scalar.copy(
+            second_grouped.rearrange("p (c j u v) -> p c u v j", j=4, u=2, v=2),
+            second_picked.rearrange("p u v (c j) -> p c u v j", j=4),
+        )
         quantize(last, second_grouped, HALF, S)
-        half_tile(1, 0, bias[:, 1:2], shared[:, 0:HALF])
+        half_tile(2, 0, bias[:, 2:3], shared[:, HALF:S])
         for m in range(SPLIT_TILES):
-            half_tile(m, 1, bias[:, m : m + 1], half_sums[:, 1 + m, :])
+            half_tile(m, 1, bias[:, m : m + 1], half_sums[:, 2 + m, :])
             store(m)
         for m in range(SPLIT_TILES, M_TILES):
             bank = whole_psum.tile([P, S], F32, name="whole_bank")

@@ -22,7 +22,9 @@ PASSES = K // (P * PACK)
 M_TILES = M // P
 HALF = S // 2
 GROUP_N = 128
-SPLIT_TILES = 3
+SPLIT_TILES = 4
+EARLY_TILES = 2
+ROW = S + HALF
 WINDOWS = 4
 
 
@@ -39,8 +41,8 @@ def tile_list_hboth_bias_kernel(tc, xT, w_words, w_scales, wgt, b, wgo, offs, of
 
         weight = keep.tile([P, S], F32, name="weight")
         planes = [keep.tile([P, T], F32, name=f"plane{n}", tag=f"slot{n}") for n in range(PASSES * PACK)]
-        early_words = keep.tile([P, PASSES, 2 * P * SPLIT_TILES], U8, name="early_words", align_bytes=64)
-        late_words = keep.tile([P, PASSES, 2 * P * (M_TILES - SPLIT_TILES)], U8, name="late_words", align_bytes=64)
+        early_words = keep.tile([P, PASSES, 2 * P * EARLY_TILES], U8, name="early_words", align_bytes=64)
+        late_words = keep.tile([P, PASSES, 2 * P * (M_TILES - EARLY_TILES)], U8, name="late_words", align_bytes=64)
         scales = keep.tile([P, PASSES, M], U8, name="scales", align_bytes=64)
         factor = keep.tile([P, S], F32, name="factor")
         windows = [keep.tile([P, T], F32, name=f"window{n}") for n in range(2)]
@@ -52,12 +54,11 @@ def tile_list_hboth_bias_kernel(tc, xT, w_words, w_scales, wgt, b, wgo, offs, of
         code_scales = [keep.tile([P, S], U8, name=f"code_scales{a}", align_bytes=64) for a in range(PASSES)]
         first_grouped = keep.tile([P, PACK * HALF], BF16, name="first_grouped", align_bytes=64)
         half_sums = keep.tile([P, 2 + SPLIT_TILES, HALF], F32, name="half_sums")
-        shared = keep.tile([P, PACK * S], F32, name="shared")
+        shared = keep.tile([P, PACK * ROW], F32, name="shared")
         second_words = keep.tile([P, 2 * HALF], F32, name="second_words", align_bytes=64)
 
-        last_picked = shared[:].rearrange("p (i j) -> p i j", i=PACK)
-        first_picked = last_picked[:, :, 0:HALF]
-        second_picked = shared[:, HALF : 7 * HALF].rearrange("p (u v j) -> p u v j", u=2, v=3)[:, :, ::2, :]
+        rows = shared[:].rearrange("p (i j) -> p i j", i=PACK)
+        second_picked = shared[:, HALF : HALF + 3 * ROW].rearrange("p (u v j) -> p u v j", u=2, v=3)[:, :, ::2, 0:HALF]
         last_weight = second_picked[:, 0, 1, 0:GROUP_N]
         second_grouped = second_words[:].bitcast(BF16)
         first_bias = second_words[:, 0:2]
@@ -79,10 +80,10 @@ def tile_list_hboth_bias_kernel(tc, xT, w_words, w_scales, wgt, b, wgo, offs, of
                 scales_view[:, 4 * q : 4 * q + 4, :].rearrange("a r n -> r a n"),
             )
         words_view = w_words.bitcast(I32).rearrange("a p n -> p a n")
-        nc.sync.dma_start(early_words[:].bitcast(I32), words_view[:, :, 0 : SPLIT_TILES * P // 2])
+        nc.sync.dma_start(early_words[:].bitcast(I32), words_view[:, :, 0 : EARLY_TILES * P // 2])
         nc.sync.dma_start(scatter_list[:], offs2)
         nc.sync.dma_start(factor[:], wgo)
-        nc.sync.dma_start(late_words[:].bitcast(I32), words_view[:, :, SPLIT_TILES * P // 2 : M // 2])
+        nc.sync.dma_start(late_words[:].bitcast(I32), words_view[:, :, EARLY_TILES * P // 2 : M // 2])
 
         nc.gpsimd.memset(bias_rows[:], 0.0)
         nc.scalar.dma_start(bias_rows[0:M_TILES, :], b.rearrange("(m p) -> m p", p=P))
@@ -104,6 +105,12 @@ def tile_list_hboth_bias_kernel(tc, xT, w_words, w_scales, wgt, b, wgo, offs, of
                 picked.rearrange("p i (c j) -> p c i j", j=4),
             )
 
+        def interleave_pairs(grouped, picked):
+            nc.scalar.copy(
+                grouped.rearrange("p (c j u v) -> p c u v j", j=4, u=2, v=2),
+                picked.rearrange("p u v (c j) -> p c u v j", j=4),
+            )
+
         def quantize(a, grouped, c0, c1):
             nc.vector.quantize_mx(out=codes[a][:, c0:c1].bitcast(E4M3X4), scales=code_scales[a][:, c0:c1], in_=grouped)
 
@@ -122,25 +129,25 @@ def tile_list_hboth_bias_kernel(tc, xT, w_words, w_scales, wgt, b, wgo, offs, of
         for n in range(WINDOWS - 2):
             windows.append(keep.tile([P, T], F32, name=f"late_window{n}", tag=f"slot{n}"))
             nc.gpsimd.memset(windows[-1][:].bitcast(I32), 0)
-        gather(last_picked[:, 0, :], last * PACK, 0, S, weight[:])
+        gather(rows[:, 0, 0:S], last * PACK, 0, S, weight[:])
         for i in range(1, PACK - 1):
-            gather(first_picked[:, i, :], last * PACK + i, 0, HALF, weight[:, 0:HALF])
-        gather(first_picked[:, PACK - 1, 0:GROUP_N], len(planes) - 1, 0, GROUP_N, chunk_weight[:])
-        gather(first_picked[:, PACK - 1, GROUP_N:HALF], len(planes) - 1, GROUP_N, HALF, last_weight)
+            gather(rows[:, i, 0:HALF], last * PACK + i, 0, HALF, weight[:, 0:HALF])
+        gather(rows[:, 3, 0:GROUP_N], len(planes) - 1, 0, GROUP_N, chunk_weight[:])
+        gather(rows[:, 3, GROUP_N:HALF], len(planes) - 1, GROUP_N, HALF, last_weight)
         codes[1] = keep.tile([P, S], U32, name="codes1", tag="held", align_bytes=64)
         quantize(1, grouped[:], 0, S)
         for c0 in range(0, HALF, GROUP_N):
             chunk = first_grouped[:, PACK * c0 : PACK * (c0 + GROUP_N)]
-            interleave(chunk, first_picked[:, :, c0 : c0 + GROUP_N])
+            interleave(chunk, rows[:, :, c0 : c0 + GROUP_N])
             quantize(last, chunk, c0, c0 + GROUP_N)
         for i in range(1, PACK):
             gather(second_picked[:, i // 2, i % 2, :], last * PACK + i, HALF, S, weight[:, HALF:S])
 
         def multiply(product, m, a, c0, c1, start, stop):
-            if m < SPLIT_TILES:
+            if m < EARLY_TILES:
                 lhsT = early_words[:, a, 2 * P * m : 2 * P * (m + 1)]
             else:
-                lhsT = late_words[:, a, 2 * P * (m - SPLIT_TILES) : 2 * P * (m - SPLIT_TILES + 1)]
+                lhsT = late_words[:, a, 2 * P * (m - EARLY_TILES) : 2 * P * (m - EARLY_TILES + 1)]
             nc.tensor.matmul_mx(
                 out=product,
                 lhsT=lhsT.bitcast(E2M1X4),
@@ -171,18 +178,17 @@ def tile_list_hboth_bias_kernel(tc, xT, w_words, w_scales, wgt, b, wgo, offs, of
             scatter(m, sums, h * HALF, (h + 1) * HALF)
 
         for c0 in range(0, HALF, GROUP_N):
-            bank = whole_psum.tile([P, S], F32, name="whole_bank")
-            for a in range(PASSES):
-                multiply(bank[:, 0:GROUP_N], 0, a, c0, c0 + GROUP_N, start=(a == 0), stop=(a == last))
-            nc.scalar.activation(half_sums[:, 0, c0 : c0 + GROUP_N], bank[:, 0:GROUP_N], IDENTITY, bias=first_bias[:, 0:1])
-        scatter(0, half_sums[:, 0, :], 0, HALF)
-        half_tile(1, 0, first_bias[:, 1:2], half_sums[:, 1, :])
-        nc.scalar.copy(
-            second_grouped.rearrange("p (c j u v) -> p c u v j", j=4, u=2, v=2),
-            second_picked.rearrange("p u v (c j) -> p c u v j", j=4),
-        )
+            for m in range(2):
+                bank = whole_psum.tile([P, S], F32, name="whole_bank")
+                for a in range(PASSES):
+                    multiply(bank[:, 0:GROUP_N], m, a, c0, c0 + GROUP_N, start=(a == 0), stop=(a == last))
+                sums = half_sums[:, m, c0 : c0 + GROUP_N]
+                nc.scalar.activation(sums, bank[:, 0:GROUP_N], IDENTITY, bias=first_bias[:, m : m + 1])
+                scatter(m, sums, c0, c0 + GROUP_N)
+        interleave_pairs(second_grouped, second_picked)
         quantize(last, second_grouped, HALF, S)
-        half_tile(2, 0, bias[:, 2:3], shared[:, HALF:S])
+        for v in range(2):
+            half_tile(2 + v, 0, bias[:, 2 + v : 3 + v], second_picked[:, 0, v, :])
         for m in range(SPLIT_TILES):
             half_tile(m, 1, bias[:, m : m + 1], half_sums[:, 2 + m, :])
             store(m)

@@ -1,5 +1,4 @@
 import concourse.mybir as mybir
-from concourse.masks import make_identity
 
 K, M, T, S = 1536, 1024, 1024, 512
 
@@ -22,10 +21,10 @@ PASSES = K // (P * PACK)
 M_TILES = M // P
 HALF = S // 2
 GROUP_N = 128
-SPLIT_TILES = 4
+SPLIT_TILES = 3
 EARLY_TILES = 2
 ROW = S + HALF
-WINDOWS = 4
+WINDOWS = 3
 
 
 def tile_list_hboth_bias_kernel(tc, xT, w_words, w_scales, wgt, b, wgo, offs, offs2, out):
@@ -40,14 +39,12 @@ def tile_list_hboth_bias_kernel(tc, xT, w_words, w_scales, wgt, b, wgo, offs, of
         scatter_list = lists.tile([P, S // 16], U16, name="scatter_list")
 
         weight = keep.tile([P, S], F32, name="weight")
-        planes = [keep.tile([P, T], F32, name=f"plane{n}", tag=f"slot{n}") for n in range(PASSES * PACK)]
+        planes = [keep.tile([P, T], F32, name=f"plane{n}") for n in range(PASSES * PACK)]
         early_words = keep.tile([P, PASSES, 2 * P * EARLY_TILES], U8, name="early_words", align_bytes=64)
         late_words = keep.tile([P, PASSES, 2 * P * (M_TILES - EARLY_TILES)], U8, name="late_words", align_bytes=64)
         scales = keep.tile([P, PASSES, M], U8, name="scales", align_bytes=64)
         factor = keep.tile([P, S], F32, name="factor")
-        windows = [keep.tile([P, T], F32, name=f"window{n}") for n in range(2)]
-        bias_rows = keep.tile([P, P], F32, name="bias_rows")
-        identity = keep.tile([P, P], F32, name="identity")
+        windows = [keep.tile([P, T], F32, name=f"window{n}") for n in range(WINDOWS)]
         bias = keep.tile([P, M_TILES], F32, name="bias")
         chunk_weight = keep.tile([P, GROUP_N], F32, name="chunk_weight", tag="held", align_bytes=64)
         codes = {a: keep.tile([P, S], U32, name=f"codes{a}", align_bytes=64) for a in (0, 2)}
@@ -66,33 +63,29 @@ def tile_list_hboth_bias_kernel(tc, xT, w_words, w_scales, wgt, b, wgo, offs, of
         x_view = xT.rearrange("(a p i) t -> a i p t", p=P, i=PACK)
         nc.sync.dma_start(gather_list[:], offs)
         nc.sync.dma_start(planes[0][:], x_view[0, 0])
-        for h in range(2):
-            nc.sync.dma_start(weight[:, h * HALF : (h + 1) * HALF], wgt[:, h * HALF : (h + 1) * HALF])
+        nc.sync.dma_start(weight[:], wgt)
         for n in range(1, PASSES * PACK):
             nc.sync.dma_start(planes[n][:], x_view[n // PACK, n % PACK])
         for window in windows:
             nc.vector.memset(window[:].bitcast(I32), 0)
         nc.vector.memset(scales[:].rearrange("p a n -> p (a n)").bitcast(I32), 0)
         scales_view = w_scales.bitcast(I32)
-        for q in range(4):
+        for r in range(4):
             nc.sync.dma_start(
-                scales[32 * q : 32 * q + 4, :, :].bitcast(I32),
-                scales_view[:, 4 * q : 4 * q + 4, :].rearrange("a r n -> r a n"),
+                scales[r:P:32, :, :].bitcast(I32),
+                scales_view[:, r:16:4, :].rearrange("a q n -> q a n"),
             )
         words_view = w_words.bitcast(I32).rearrange("a p n -> p a n")
         nc.sync.dma_start(early_words[:].bitcast(I32), words_view[:, :, 0 : EARLY_TILES * P // 2])
+        bias_view = b.rearrange("(m p) -> p m", p=P)
+        with nc.allow_non_contiguous_dma(reason="one bias value a partition and row tile"):
+            nc.sync.dma_start(first_bias, bias_view[:, 0:2])
         nc.sync.dma_start(scatter_list[:], offs2)
         nc.sync.dma_start(factor[:], wgo)
         nc.sync.dma_start(late_words[:].bitcast(I32), words_view[:, :, EARLY_TILES * P // 2 : M // 2])
+        with nc.allow_non_contiguous_dma(reason="one bias value a partition and row tile"):
+            nc.sync.dma_start(bias[:], bias_view)
 
-        nc.gpsimd.memset(bias_rows[:], 0.0)
-        nc.scalar.dma_start(bias_rows[0:M_TILES, :], b.rearrange("(m p) -> m p", p=P))
-        make_identity(nc, identity[:])
-
-        turned = whole_psum.tile([P, S], F32, name="whole_bank")
-        nc.tensor.transpose(turned[:, 0:P], bias_rows[:], identity[:])
-        nc.scalar.copy(bias[:], turned[:, 0:M_TILES])
-        nc.scalar.copy(first_bias, turned[:, 0:2])
         nc.scalar.copy(chunk_weight[:], weight[:, 0:GROUP_N])
         nc.scalar.copy(last_weight, weight[:, GROUP_N:HALF])
 
@@ -119,16 +112,13 @@ def tile_list_hboth_bias_kernel(tc, xT, w_words, w_scales, wgt, b, wgo, offs, of
             picked = work.tile([P, PACK, S], F32, name="picked")
             grouped = work.tile([P, S * PACK], BF16, name="grouped", align_bytes=64)
             for i in range(PACK):
-                for c0, c1 in ((0, HALF), (HALF, S)) if a == i == 0 or i == PACK - 1 else ((0, S),):
+                for c0, c1 in ((0, HALF), (HALF, S)) if i == PACK - 1 else ((0, S),):
                     gather(picked[:, i, c0:c1], a * PACK + i, c0, c1, weight[:, c0:c1])
             for c0 in (0, HALF):
                 interleave(grouped[:, PACK * c0 : PACK * (c0 + HALF)], picked[:, :, c0 : c0 + HALF])
             if a == 0:
                 quantize(a, grouped[:], 0, S)
 
-        for n in range(WINDOWS - 2):
-            windows.append(keep.tile([P, T], F32, name=f"late_window{n}", tag=f"slot{n}"))
-            nc.gpsimd.memset(windows[-1][:].bitcast(I32), 0)
         gather(rows[:, 0, 0:S], last * PACK, 0, S, weight[:])
         for i in range(1, PACK - 1):
             gather(rows[:, i, 0:HALF], last * PACK + i, 0, HALF, weight[:, 0:HALF])
@@ -187,7 +177,7 @@ def tile_list_hboth_bias_kernel(tc, xT, w_words, w_scales, wgt, b, wgo, offs, of
                 scatter(m, sums, c0, c0 + GROUP_N)
         interleave_pairs(second_grouped, second_picked)
         quantize(last, second_grouped, HALF, S)
-        for v in range(2):
+        for v in range(SPLIT_TILES - 2):
             half_tile(2 + v, 0, bias[:, 2 + v : 3 + v], second_picked[:, 0, v, :])
         for m in range(SPLIT_TILES):
             half_tile(m, 1, bias[:, m : m + 1], half_sums[:, 2 + m, :])

@@ -18,13 +18,13 @@ IDENTITY = mybir.ActivationFunctionType.Identity
 P = 128
 PACK = 4
 PASSES = K // (P * PACK)
+PLANES = PASSES * PACK
 M_TILES = M // P
 HALF = S // 2
-GROUP_N = 128
-SPLIT_TILES = 3
-EARLY_TILES = 2
-ROW = S + HALF
+CHUNK = 128
+CHUNK_TILES = 2
 WINDOWS = 3
+CELL = HALF + CHUNK
 
 
 def tile_list_hboth_bias_kernel(tc, xT, w_words, w_scales, wgt, b, wgo, offs, offs2, out):
@@ -33,38 +33,39 @@ def tile_list_hboth_bias_kernel(tc, xT, w_words, w_scales, wgt, b, wgo, offs, of
         tc.tile_pool(name="lists", bufs=1) as lists,
         tc.tile_pool(name="keep", bufs=1) as keep,
         tc.tile_pool(name="work", bufs=2) as work,
-        tc.psum_pool(name="whole_psum", bufs=2) as whole_psum,
+        tc.psum_pool(name="banks", bufs=3) as banks,
     ):
         gather_list = lists.tile([P, S // 16], U16, name="gather_list")
         scatter_list = lists.tile([P, S // 16], U16, name="scatter_list")
 
         weight = keep.tile([P, S], F32, name="weight")
-        planes = [keep.tile([P, T], F32, name=f"plane{n}") for n in range(PASSES * PACK)]
-        early_words = keep.tile([P, PASSES, 2 * P * EARLY_TILES], U8, name="early_words", align_bytes=64)
-        late_words = keep.tile([P, PASSES, 2 * P * (M_TILES - EARLY_TILES)], U8, name="late_words", align_bytes=64)
+        planes = [keep.tile([P, T], F32, name=f"plane{n}") for n in range(PLANES)]
+        early_words = keep.tile([P, PASSES, 2 * P * CHUNK_TILES], U8, name="early_words", align_bytes=64)
+        late_words = keep.tile([P, PASSES, 2 * P * (M_TILES - CHUNK_TILES)], U8, name="late_words", align_bytes=64)
         scales = keep.tile([P, PASSES, M], U8, name="scales", align_bytes=64)
         factor = keep.tile([P, S], F32, name="factor")
         windows = [keep.tile([P, T], F32, name=f"window{n}") for n in range(WINDOWS)]
         bias = keep.tile([P, M_TILES], F32, name="bias")
-        chunk_weight = keep.tile([P, GROUP_N], F32, name="chunk_weight", tag="held", align_bytes=64)
+        chunk_weight = keep.tile([P, CHUNK], F32, name="chunk_weight", tag="held", align_bytes=64)
         codes = {a: keep.tile([P, S], U32, name=f"codes{a}", align_bytes=64) for a in (0, 2)}
         code_scales = [keep.tile([P, S], U8, name=f"code_scales{a}", align_bytes=64) for a in range(PASSES)]
         first_grouped = keep.tile([P, PACK * HALF], BF16, name="first_grouped", align_bytes=64)
-        half_sums = keep.tile([P, 2 + SPLIT_TILES, HALF], F32, name="half_sums")
-        shared = keep.tile([P, PACK * ROW], F32, name="shared")
         second_words = keep.tile([P, 2 * HALF], F32, name="second_words", align_bytes=64)
+        split_sums = keep.tile([P, WINDOWS, S], F32, name="split_sums")
+        last_picked = keep.tile([P, 9 * CELL], F32, name="last_picked")
 
-        rows = shared[:].rearrange("p (i j) -> p i j", i=PACK)
-        second_picked = shared[:, HALF : HALF + 3 * ROW].rearrange("p (u v j) -> p u v j", u=2, v=3)[:, :, ::2, 0:HALF]
-        last_weight = second_picked[:, 0, 1, 0:GROUP_N]
+        early_first = last_picked[:, 0 : 2 * S].rearrange("p (v j) -> p v j", v=2)[:, :, 0:HALF]
+        late_first = last_picked[:, 3 * CELL : 9 * CELL].rearrange("p (v j) -> p v j", v=2)[:, :, 0:HALF]
+        second_picked = last_picked[:, HALF : HALF + 6 * CELL].rearrange("p (u w j) -> p u w j", u=2, w=3)[:, :, ::2, 0:HALF]
         second_grouped = second_words[:].bitcast(BF16)
-        first_bias = second_words[:, 0:2]
+        unit = second_words[:, 0:1]
 
         x_view = xT.rearrange("(a p i) t -> a i p t", p=P, i=PACK)
-        nc.sync.dma_start(gather_list[:], offs)
         nc.sync.dma_start(planes[0][:], x_view[0, 0])
-        nc.sync.dma_start(weight[:], wgt)
-        for n in range(1, PASSES * PACK):
+        nc.sync.dma_start(gather_list[:], offs)
+        for c0 in (0, HALF):
+            nc.sync.dma_start(weight[:, c0 : c0 + HALF], wgt[:, c0 : c0 + HALF])
+        for n in range(1, PLANES):
             nc.sync.dma_start(planes[n][:], x_view[n // PACK, n % PACK])
         for window in windows:
             nc.vector.memset(window[:].bitcast(I32), 0)
@@ -76,18 +77,16 @@ def tile_list_hboth_bias_kernel(tc, xT, w_words, w_scales, wgt, b, wgo, offs, of
                 scales_view[:, r:16:4, :].rearrange("a q n -> q a n"),
             )
         words_view = w_words.bitcast(I32).rearrange("a p n -> p a n")
-        nc.sync.dma_start(early_words[:].bitcast(I32), words_view[:, :, 0 : EARLY_TILES * P // 2])
         bias_view = b.rearrange("(m p) -> p m", p=P)
-        with nc.allow_non_contiguous_dma(reason="one bias value a partition and row tile"):
-            nc.sync.dma_start(first_bias, bias_view[:, 0:2])
-        nc.sync.dma_start(scatter_list[:], offs2)
-        nc.sync.dma_start(factor[:], wgo)
-        nc.sync.dma_start(late_words[:].bitcast(I32), words_view[:, :, EARLY_TILES * P // 2 : M // 2])
+        nc.sync.dma_start(early_words[:].bitcast(I32), words_view[:, :, 0 : CHUNK_TILES * P // 2])
         with nc.allow_non_contiguous_dma(reason="one bias value a partition and row tile"):
             nc.sync.dma_start(bias[:], bias_view)
+        nc.sync.dma_start(scatter_list[:], offs2)
+        nc.sync.dma_start(factor[:], wgo)
+        nc.sync.dma_start(late_words[:].bitcast(I32), words_view[:, :, CHUNK_TILES * P // 2 : M // 2])
+        nc.vector.memset(unit, 1.0)
 
-        nc.scalar.copy(chunk_weight[:], weight[:, 0:GROUP_N])
-        nc.scalar.copy(last_weight, weight[:, GROUP_N:HALF])
+        nc.scalar.copy(chunk_weight[:], weight[:, 0:CHUNK])
 
         def gather(picked, n, c0, c1, factors):
             nc.vector.tensor_tensor(picked, planes[n][:].indirect(gather_list[:, c0 // 16 : c1 // 16]), factors, MULT)
@@ -98,10 +97,10 @@ def tile_list_hboth_bias_kernel(tc, xT, w_words, w_scales, wgt, b, wgo, offs, of
                 picked.rearrange("p i (c j) -> p c i j", j=4),
             )
 
-        def interleave_pairs(grouped, picked):
+        def interleave_pair(grouped, picked, u):
             nc.scalar.copy(
-                grouped.rearrange("p (c j u v) -> p c u v j", j=4, u=2, v=2),
-                picked.rearrange("p u v (c j) -> p c u v j", j=4),
+                grouped.rearrange("p (c j u v) -> p u c v j", j=4, u=2, v=2)[:, u],
+                picked.rearrange("p v (c j) -> p c v j", j=4),
             )
 
         def quantize(a, grouped, c0, c1):
@@ -112,81 +111,73 @@ def tile_list_hboth_bias_kernel(tc, xT, w_words, w_scales, wgt, b, wgo, offs, of
             picked = work.tile([P, PACK, S], F32, name="picked")
             grouped = work.tile([P, S * PACK], BF16, name="grouped", align_bytes=64)
             for i in range(PACK):
-                for c0, c1 in ((0, HALF), (HALF, S)) if i == PACK - 1 else ((0, S),):
+                for c0, c1 in ((0, HALF), (HALF, S)) if (a, i) in ((0, 0), (0, PACK - 1)) else ((0, S),):
                     gather(picked[:, i, c0:c1], a * PACK + i, c0, c1, weight[:, c0:c1])
-            for c0 in (0, HALF):
-                interleave(grouped[:, PACK * c0 : PACK * (c0 + HALF)], picked[:, :, c0 : c0 + HALF])
             if a == 0:
+                for u in range(2):
+                    interleave_pair(grouped[:, 0 : PACK * HALF], picked[:, 2 * u : 2 * u + 2, 0:HALF], u)
+                interleave(grouped[:, PACK * HALF : PACK * S], picked[:, :, HALF:S])
                 quantize(a, grouped[:], 0, S)
+            else:
+                for u in range(2):
+                    interleave_pair(grouped[:], picked[:, 2 * u : 2 * u + 2, :], u)
 
-        gather(rows[:, 0, 0:S], last * PACK, 0, S, weight[:])
-        for i in range(1, PACK - 1):
-            gather(rows[:, i, 0:HALF], last * PACK + i, 0, HALF, weight[:, 0:HALF])
-        gather(rows[:, 3, 0:GROUP_N], len(planes) - 1, 0, GROUP_N, chunk_weight[:])
-        gather(rows[:, 3, GROUP_N:HALF], len(planes) - 1, GROUP_N, HALF, last_weight)
+        gather(last_picked[:, 0:S], PLANES - 4, 0, S, weight[:])
+        gather(early_first[:, 1, :], PLANES - 3, 0, HALF, weight[:, 0:HALF])
+        interleave_pair(first_grouped[:], early_first, 0)
+        gather(last_picked[:, 3 * CELL : 3 * CELL + S], PLANES - 2, 0, S, weight[:])
+        gather(late_first[:, 1, 0:CHUNK], PLANES - 1, 0, CHUNK, chunk_weight[:])
+        gather(late_first[:, 1, CHUNK:HALF], PLANES - 1, CHUNK, HALF, weight[:, CHUNK:HALF])
         codes[1] = keep.tile([P, S], U32, name="codes1", tag="held", align_bytes=64)
         quantize(1, grouped[:], 0, S)
-        for c0 in range(0, HALF, GROUP_N):
-            chunk = first_grouped[:, PACK * c0 : PACK * (c0 + GROUP_N)]
-            interleave(chunk, rows[:, :, c0 : c0 + GROUP_N])
-            quantize(last, chunk, c0, c0 + GROUP_N)
-        for i in range(1, PACK):
-            gather(second_picked[:, i // 2, i % 2, :], last * PACK + i, HALF, S, weight[:, HALF:S])
+        for c0 in range(0, HALF, CHUNK):
+            chunk = first_grouped[:, PACK * c0 : PACK * (c0 + CHUNK)]
+            interleave_pair(chunk, late_first[:, :, c0 : c0 + CHUNK], 1)
+            quantize(last, chunk, c0, c0 + CHUNK)
+        for u in range(2):
+            gather(second_picked[:, u, 1, :], last * PACK + 2 * u + 1, HALF, S, weight[:, HALF:S])
 
-        def multiply(product, m, a, c0, c1, start, stop):
-            if m < EARLY_TILES:
-                lhsT = early_words[:, a, 2 * P * m : 2 * P * (m + 1)]
+        def products(m, c0, c1, scale, sums):
+            if m < CHUNK_TILES:
+                words, column = early_words, m
             else:
-                lhsT = late_words[:, a, 2 * P * (m - EARLY_TILES) : 2 * P * (m - EARLY_TILES + 1)]
-            nc.tensor.matmul_mx(
-                out=product,
-                lhsT=lhsT.bitcast(E2M1X4),
-                lhsT_scale=scales[:, a, P * m : P * (m + 1)],
-                rhs=codes[a][:, c0:c1].bitcast(E4M3X4),
-                rhs_scale=code_scales[a][:, c0:c1],
-                start=start,
-                stop=stop,
-            )
-
-        def scatter(m, sums, c0, c1):
-            nc.vector.tensor_tensor(
-                windows[m % WINDOWS][:].indirect(scatter_list[:, c0 // 16 : c1 // 16]), sums, factor[:, c0:c1], MULT
-            )
-
-        def store(m):
-            nc.sync.dma_start(out[P * m : P * (m + 1), :], windows[m % WINDOWS][:])
-
-        def half_tile(m, h, bias_column, sums):
-            bank = whole_psum.tile([P, S], F32, name="whole_bank")
+                words, column = late_words, m - CHUNK_TILES
+            bank = banks.tile([P, S], F32, name="bank")
+            width = S if c1 - c0 == S else CHUNK
             for a in range(PASSES):
-                for c in range(0, HALF, GROUP_N):
-                    multiply(
-                        bank[:, c : c + GROUP_N], m, a, h * HALF + c, h * HALF + c + GROUP_N,
-                        start=(a == 0 and c == 0), stop=(a == last and c == HALF - GROUP_N),
+                for c in range(c0, c1, width):
+                    nc.tensor.matmul_mx(
+                        out=bank[:, c - c0 : c - c0 + width],
+                        lhsT=words[:, a, 2 * P * column : 2 * P * (column + 1)].bitcast(E2M1X4),
+                        lhsT_scale=scales[:, a, P * m : P * (m + 1)],
+                        rhs=codes[a][:, c : c + width].bitcast(E4M3X4),
+                        rhs_scale=code_scales[a][:, c : c + width],
+                        start=(a == 0 and c == c0),
+                        stop=(a == last and c == c1 - width),
                     )
-            nc.scalar.activation(sums, bank[:, 0:HALF], IDENTITY, bias=bias_column)
-            scatter(m, sums, h * HALF, (h + 1) * HALF)
+            nc.scalar.activation(sums, bank[:, 0 : c1 - c0], IDENTITY, bias=bias[:, m : m + 1], scale=scale)
 
-        for c0 in range(0, HALF, GROUP_N):
-            for m in range(2):
-                bank = whole_psum.tile([P, S], F32, name="whole_bank")
-                for a in range(PASSES):
-                    multiply(bank[:, 0:GROUP_N], m, a, c0, c0 + GROUP_N, start=(a == 0), stop=(a == last))
-                sums = half_sums[:, m, c0 : c0 + GROUP_N]
-                nc.scalar.activation(sums, bank[:, 0:GROUP_N], IDENTITY, bias=first_bias[:, m : m + 1])
-                scatter(m, sums, c0, c0 + GROUP_N)
-        interleave_pairs(second_grouped, second_picked)
-        quantize(last, second_grouped, HALF, S)
-        for v in range(SPLIT_TILES - 2):
-            half_tile(2 + v, 0, bias[:, 2 + v : 3 + v], second_picked[:, 0, v, :])
-        for m in range(SPLIT_TILES):
-            half_tile(m, 1, bias[:, m : m + 1], half_sums[:, 2 + m, :])
-            store(m)
-        for m in range(SPLIT_TILES, M_TILES):
-            bank = whole_psum.tile([P, S], F32, name="whole_bank")
-            for a in range(PASSES):
-                multiply(bank[:], m, a, 0, S, start=(a == 0), stop=(a == last))
+        def row_tile(m, c0, c1, scale, sums):
+            step = CHUNK if m == 0 else c1 - c0
+            for c in range(c0, c1, step):
+                products(m, c, c + step, scale, sums[:, c - c0 : c - c0 + step])
+            window = windows[m % WINDOWS]
+            nc.vector.tensor_tensor(window[:].indirect(scatter_list[:, c0 // 16 : c1 // 16]), sums, factor[:, c0:c1], MULT)
+            if c1 == S:
+                nc.sync.dma_start(out[P * m : P * (m + 1), :], window[:])
+
+        cuts = (HALF, CHUNK, HALF)
+        for m in (1, 0):
+            row_tile(m, 0, cuts[m], unit, split_sums[:, m, 0 : cuts[m]])
+        nc.scalar.copy(
+            second_grouped.rearrange("p (c j u v) -> p c u v j", j=4, u=2, v=2),
+            second_picked.rearrange("p u v (c j) -> p c u v j", j=4),
+        )
+        for c0 in range(HALF, S, CHUNK):
+            quantize(last, second_grouped[:, PACK * (c0 - HALF) : PACK * (c0 - HALF + CHUNK)], c0, c0 + CHUNK)
+        row_tile(WINDOWS - 1, 0, HALF, 1.0, second_picked[:, 1, 0, :])
+        for m in range(WINDOWS):
+            row_tile(m, cuts[m], S, 1.0, split_sums[:, m, cuts[m] : S])
+        for m in range(WINDOWS, M_TILES):
             sums = work.tile([P, S], F32, name="sums")
-            nc.scalar.activation(sums[:], bank[:], IDENTITY, bias=bias[:, m : m + 1])
-            scatter(m, sums[:], 0, S)
-            store(m)
+            row_tile(m, 0, S, 1.0, sums[:])

@@ -50,15 +50,15 @@ def tile_list_hboth_bias_kernel(tc, xT, w_words, w_scales, wgt, b, wgo, offs, of
         codes = {a: keep.tile([P, S], U32, name=f"codes{a}", align_bytes=64) for a in (0, 2)}
         code_scales = [keep.tile([P, S], U8, name=f"code_scales{a}", align_bytes=64) for a in range(PASSES)]
         first_grouped = keep.tile([P, PACK * HALF], BF16, name="first_grouped", align_bytes=64)
-        second_words = keep.tile([P, 2 * HALF], F32, name="second_words", align_bytes=64)
         split_sums = keep.tile([P, WINDOWS, S], F32, name="split_sums")
-        last_picked = keep.tile([P, 9 * CELL], F32, name="last_picked")
+        last_picked = keep.tile([P, 9 * CELL], F32, name="last_picked", align_bytes=64)
 
         early_first = last_picked[:, 0 : 2 * S].rearrange("p (v j) -> p v j", v=2)[:, :, 0:HALF]
         late_first = last_picked[:, 3 * CELL : 9 * CELL].rearrange("p (v j) -> p v j", v=2)[:, :, 0:HALF]
         second_picked = last_picked[:, HALF : HALF + 6 * CELL].rearrange("p (u w j) -> p u w j", u=2, w=3)[:, :, ::2, 0:HALF]
-        second_grouped = second_words[:].bitcast(BF16)
-        unit = second_words[:, 0:1]
+        second_words = last_picked[:, 6 * CELL + CHUNK : 6 * CELL + CHUNK + S]
+        second_grouped = second_words.bitcast(BF16)
+        first_bias = second_words[:, 0:CHUNK_TILES]
 
         x_view = xT.rearrange("(a p i) t -> a i p t", p=P, i=PACK)
         nc.sync.dma_start(planes[0][:], x_view[0, 0])
@@ -84,7 +84,6 @@ def tile_list_hboth_bias_kernel(tc, xT, w_words, w_scales, wgt, b, wgo, offs, of
         nc.sync.dma_start(scatter_list[:], offs2)
         nc.sync.dma_start(factor[:], wgo)
         nc.sync.dma_start(late_words[:].bitcast(I32), words_view[:, :, CHUNK_TILES * P // 2 : M // 2])
-        nc.vector.memset(unit, 1.0)
 
         nc.scalar.copy(chunk_weight[:], weight[:, 0:CHUNK])
 
@@ -114,9 +113,8 @@ def tile_list_hboth_bias_kernel(tc, xT, w_words, w_scales, wgt, b, wgo, offs, of
                 for c0, c1 in ((0, HALF), (HALF, S)) if (a, i) in ((0, 0), (0, PACK - 1)) else ((0, S),):
                     gather(picked[:, i, c0:c1], a * PACK + i, c0, c1, weight[:, c0:c1])
             if a == 0:
-                for u in range(2):
-                    interleave_pair(grouped[:, 0 : PACK * HALF], picked[:, 2 * u : 2 * u + 2, 0:HALF], u)
-                interleave(grouped[:, PACK * HALF : PACK * S], picked[:, :, HALF:S])
+                for c0 in (0, HALF):
+                    interleave(grouped[:, PACK * c0 : PACK * (c0 + HALF)], picked[:, :, c0 : c0 + HALF])
                 quantize(a, grouped[:], 0, S)
             else:
                 for u in range(2):
@@ -134,10 +132,11 @@ def tile_list_hboth_bias_kernel(tc, xT, w_words, w_scales, wgt, b, wgo, offs, of
             chunk = first_grouped[:, PACK * c0 : PACK * (c0 + CHUNK)]
             interleave_pair(chunk, late_first[:, :, c0 : c0 + CHUNK], 1)
             quantize(last, chunk, c0, c0 + CHUNK)
+        nc.scalar.copy(first_bias, bias[:, 0:CHUNK_TILES])
         for u in range(2):
             gather(second_picked[:, u, 1, :], last * PACK + 2 * u + 1, HALF, S, weight[:, HALF:S])
 
-        def products(m, c0, c1, scale, sums):
+        def products(m, c0, c1, columns, sums):
             if m < CHUNK_TILES:
                 words, column = early_words, m
             else:
@@ -155,12 +154,12 @@ def tile_list_hboth_bias_kernel(tc, xT, w_words, w_scales, wgt, b, wgo, offs, of
                         start=(a == 0 and c == c0),
                         stop=(a == last and c == c1 - width),
                     )
-            nc.scalar.activation(sums, bank[:, 0 : c1 - c0], IDENTITY, bias=bias[:, m : m + 1], scale=scale)
+            nc.scalar.activation(sums, bank[:, 0 : c1 - c0], IDENTITY, bias=columns[:, m : m + 1])
 
-        def row_tile(m, c0, c1, scale, sums):
+        def row_tile(m, c0, c1, columns, sums):
             step = CHUNK if m == 0 else c1 - c0
             for c in range(c0, c1, step):
-                products(m, c, c + step, scale, sums[:, c - c0 : c - c0 + step])
+                products(m, c, c + step, columns, sums[:, c - c0 : c - c0 + step])
             window = windows[m % WINDOWS]
             nc.vector.tensor_tensor(window[:].indirect(scatter_list[:, c0 // 16 : c1 // 16]), sums, factor[:, c0:c1], MULT)
             if c1 == S:
@@ -168,16 +167,16 @@ def tile_list_hboth_bias_kernel(tc, xT, w_words, w_scales, wgt, b, wgo, offs, of
 
         cuts = (HALF, CHUNK, HALF)
         for m in (1, 0):
-            row_tile(m, 0, cuts[m], unit, split_sums[:, m, 0 : cuts[m]])
+            row_tile(m, 0, cuts[m], first_bias, split_sums[:, m, 0 : cuts[m]])
         nc.scalar.copy(
             second_grouped.rearrange("p (c j u v) -> p c u v j", j=4, u=2, v=2),
             second_picked.rearrange("p u v (c j) -> p c u v j", j=4),
         )
         for c0 in range(HALF, S, CHUNK):
             quantize(last, second_grouped[:, PACK * (c0 - HALF) : PACK * (c0 - HALF + CHUNK)], c0, c0 + CHUNK)
-        row_tile(WINDOWS - 1, 0, HALF, 1.0, second_picked[:, 1, 0, :])
+        row_tile(WINDOWS - 1, 0, HALF, bias, second_picked[:, 1, 0, :])
         for m in range(WINDOWS):
-            row_tile(m, cuts[m], S, 1.0, split_sums[:, m, cuts[m] : S])
+            row_tile(m, cuts[m], S, bias, split_sums[:, m, cuts[m] : S])
         for m in range(WINDOWS, M_TILES):
             sums = work.tile([P, S], F32, name="sums")
-            row_tile(m, 0, S, 1.0, sums[:])
+            row_tile(m, 0, S, bias, sums[:])

@@ -1,4 +1,5 @@
 import concourse.mybir as mybir
+from concourse.masks import make_identity
 
 K, M, T, S = 1536, 1024, 1024, 512
 
@@ -14,6 +15,7 @@ E4M3X4 = mybir.dt.float8_e4m3fn_x4
 E2M1X4 = mybir.dt.float4_e2m1fn_x4
 MULT = mybir.AluOpType.mult
 IDENTITY = mybir.ActivationFunctionType.Identity
+COPY = mybir.ActivationFunctionType.Copy
 
 P = 128
 PACK = 4
@@ -25,6 +27,9 @@ CHUNK = 128
 CHUNK_TILES = 2
 WINDOWS = 3
 CELL = HALF + CHUNK
+GROUPS = 8
+GROUP = P // GROUPS
+BLOCKS = S // P
 
 
 def tile_list_hboth_bias_kernel(tc, xT, w_words, w_scales, wgt, b, wgo, offs, offs2, out):
@@ -34,11 +39,16 @@ def tile_list_hboth_bias_kernel(tc, xT, w_words, w_scales, wgt, b, wgo, offs, of
         tc.tile_pool(name="keep", bufs=1) as keep,
         tc.tile_pool(name="work", bufs=2) as work,
         tc.psum_pool(name="banks", bufs=3) as banks,
+        tc.psum_pool(name="turns", bufs=1) as turns,
     ):
         gather_list = lists.tile([P, S // 16], U16, name="gather_list")
         scatter_list = lists.tile([P, S // 16], U16, name="scatter_list")
 
         weight = keep.tile([P, S], F32, name="weight")
+        identity = keep.tile([P, P], F32, name="identity")
+        weight_rows = keep.tile([P, P], F32, name="weight_rows")
+        token_weight = keep.tile([P, S], F32, name="token_weight")
+        token_pairs = keep.tile([P, 2 * S], BF16, name="token_pairs")
         planes = [keep.tile([P, T], F32, name=f"plane{n}") for n in range(PLANES)]
         early_words = keep.tile([P, PASSES, 2 * P * CHUNK_TILES], U8, name="early_words", align_bytes=64)
         late_words = keep.tile([P, PASSES, 2 * P * (M_TILES - CHUNK_TILES)], U8, name="late_words", align_bytes=64)
@@ -48,7 +58,8 @@ def tile_list_hboth_bias_kernel(tc, xT, w_words, w_scales, wgt, b, wgo, offs, of
         bias = keep.tile([P, M_TILES], F32, name="bias")
         chunk_weight = keep.tile([P, CHUNK], F32, name="chunk_weight", tag="held", align_bytes=64)
         codes = {a: keep.tile([P, S], U32, name=f"codes{a}", align_bytes=64) for a in (0, 2)}
-        code_scales = [keep.tile([P, S], U8, name=f"code_scales{a}", align_bytes=64) for a in range(PASSES)]
+        early_chunk_weight = keep.tile([P, CHUNK], F32, name="early_chunk_weight", tag="early_held", align_bytes=64)
+        code_scales = {a: keep.tile([P, S], U8, name=f"code_scales{a}", align_bytes=64) for a in (1, 2)}
         first_grouped = keep.tile([P, PACK * HALF], BF16, name="first_grouped", align_bytes=64)
         split_sums = keep.tile([P, WINDOWS, S], F32, name="split_sums")
         last_picked = keep.tile([P, 9 * CELL], F32, name="last_picked", align_bytes=64)
@@ -61,12 +72,12 @@ def tile_list_hboth_bias_kernel(tc, xT, w_words, w_scales, wgt, b, wgo, offs, of
         first_bias = second_words[:, 0:CHUNK_TILES]
 
         x_view = xT.rearrange("(a p i) t -> a i p t", p=P, i=PACK)
+        nc.sync.dma_start(weight_rows[:], wgt.rearrange("(g r) (c j) -> (r c) g j", g=GROUPS, c=BLOCKS)[0:GROUP])
         nc.sync.dma_start(planes[0][:], x_view[0, 0])
         nc.sync.dma_start(gather_list[:], offs)
-        for c0 in (0, HALF):
-            nc.sync.dma_start(weight[:, c0 : c0 + HALF], wgt[:, c0 : c0 + HALF])
         for n in range(1, PLANES):
             nc.sync.dma_start(planes[n][:], x_view[n // PACK, n % PACK])
+        make_identity(nc, identity[:])
         for window in windows:
             nc.vector.memset(window[:].bitcast(I32), 0)
         nc.vector.memset(scales[:].rearrange("p a n -> p (a n)").bitcast(I32), 0)
@@ -82,19 +93,28 @@ def tile_list_hboth_bias_kernel(tc, xT, w_words, w_scales, wgt, b, wgo, offs, of
         with nc.allow_non_contiguous_dma(reason="one bias value a partition and row tile"):
             nc.sync.dma_start(bias[:], bias_view)
         nc.sync.dma_start(scatter_list[:], offs2)
-        nc.sync.dma_start(factor[:], wgo)
+        for c0 in (0, HALF):
+            nc.sync.dma_start(factor[:, c0 : c0 + HALF], wgo[:, c0 : c0 + HALF])
         nc.sync.dma_start(late_words[:].bitcast(I32), words_view[:, :, CHUNK_TILES * P // 2 : M // 2])
 
-        nc.scalar.copy(chunk_weight[:], weight[:, 0:CHUNK])
+        turned_rows = turns.tile([P, P], F32, name="turned_rows", tag="turn2")
+        nc.tensor.transpose(turned_rows[:], weight_rows[:], identity[:])
+        for h in range(2):
+            nc.scalar.copy(
+                token_weight[:, HALF * h : HALF * (h + 1)].rearrange("j (n r) -> j n r", r=GROUP),
+                turned_rows[:, GROUP * h : GROUP * (h + 1)].unsqueeze(2).to_broadcast([P, GROUP, GROUP]),
+            )
+        for h in range(2):
+            spread = turns.tile([P, HALF], F32, name="spread", tag=f"turn{1 - h}")
+            for c in range(2):
+                c0 = HALF * h + P * c
+                nc.tensor.transpose(spread[:, P * c : P * (c + 1)], token_weight[:, c0 : c0 + P], identity[:])
+            nc.scalar.copy(weight[:, HALF * h : HALF * (h + 1)], spread[:])
+        for held in (early_chunk_weight, chunk_weight):
+            nc.scalar.copy(held[:], weight[:, 0:CHUNK])
 
         def gather(picked, n, c0, c1, factors):
             nc.vector.tensor_tensor(picked, planes[n][:].indirect(gather_list[:, c0 // 16 : c1 // 16]), factors, MULT)
-
-        def interleave(grouped, picked):
-            nc.scalar.copy(
-                grouped.rearrange("p (c j i) -> p c i j", j=4, i=PACK),
-                picked.rearrange("p i (c j) -> p c i j", j=4),
-            )
 
         def interleave_pair(grouped, picked, u):
             nc.scalar.copy(
@@ -110,17 +130,41 @@ def tile_list_hboth_bias_kernel(tc, xT, w_words, w_scales, wgt, b, wgo, offs, of
             picked = work.tile([P, PACK, S], F32, name="picked")
             grouped = work.tile([P, S * PACK], BF16, name="grouped", align_bytes=64)
             for i in range(PACK):
-                for c0, c1 in ((0, HALF), (HALF, S)) if (a, i) in ((0, 0), (0, PACK - 1)) else ((0, S),):
-                    gather(picked[:, i, c0:c1], a * PACK + i, c0, c1, weight[:, c0:c1])
+                if a == 0 and i < 2:
+                    nc.vector.tensor_copy(picked[:, i, :], planes[i][:].indirect(gather_list[:]))
+                else:
+                    gather(picked[:, i, :], a * PACK + i, 0, S, weight[:])
             if a == 0:
-                for c0 in (0, HALF):
-                    interleave(grouped[:, PACK * c0 : PACK * (c0 + HALF)], picked[:, :, c0 : c0 + HALF])
-                quantize(a, grouped[:], 0, S)
+                by_token = [turns.tile([P, 2, 2, P], F32, name=f"by_token{h}", tag=f"turn{h}") for h in range(2)]
+                for i in range(2):
+                    for c in range(BLOCKS):
+                        nc.tensor.transpose(by_token[c // 2][:, c % 2, i, :], picked[:, i, P * c : P * (c + 1)], identity[:])
+                pair_words = turns.tile([P, S], F32, name="pair_words", tag="turn2")
+                for c in range(BLOCKS):
+                    for g in range(GROUPS):
+                        p0 = P * c + GROUP * g
+                        nc.scalar.activation(
+                            token_pairs[:, 2 * p0 : 2 * (p0 + GROUP)].rearrange("j (r i) -> j i r", i=2),
+                            by_token[c // 2][:, c % 2, :, GROUP * g : GROUP * (g + 1)],
+                            COPY,
+                            scale=token_weight[:, p0 : p0 + 1],
+                        )
+                    nc.tensor.transpose(
+                        pair_words[:, P * c : P * (c + 1)], token_pairs[:].bitcast(F32)[:, P * c : P * (c + 1)], identity[:]
+                    )
+                interleave_pair(grouped[:], picked[:, 2:4, :], 1)
+                nc.scalar.copy(grouped[:].bitcast(F32).rearrange("p (j u) -> p u j", u=2)[:, 0, :], pair_words[:])
+                opening_grouped = grouped
             else:
-                for u in range(2):
-                    interleave_pair(grouped[:], picked[:, 2 * u : 2 * u + 2, :], u)
+                nc.scalar.copy(
+                    grouped[:].rearrange("p (c j i) -> p c i j", j=4, i=PACK),
+                    picked[:].rearrange("p i (c j) -> p c i j", j=4),
+                )
 
-        gather(last_picked[:, 0:S], PLANES - 4, 0, S, weight[:])
+        gather(last_picked[:, 0:CHUNK], PLANES - 4, 0, CHUNK, early_chunk_weight[:])
+        gather(last_picked[:, CHUNK:S], PLANES - 4, CHUNK, S, weight[:, CHUNK:S])
+        code_scales[0] = keep.tile([P, S], U8, name="code_scales0", tag="early_held", align_bytes=64)
+        quantize(0, opening_grouped[:], 0, S)
         gather(early_first[:, 1, :], PLANES - 3, 0, HALF, weight[:, 0:HALF])
         interleave_pair(first_grouped[:], early_first, 0)
         gather(last_picked[:, 3 * CELL : 3 * CELL + S], PLANES - 2, 0, S, weight[:])

@@ -46,7 +46,7 @@ def tile_list_hboth_bias_kernel(tc, xT, w_words, w_scales, wgt, b, wgo, offs, of
 
         weight = keep.tile([P, S], F32, name="weight")
         identity = keep.tile([P, P], F32, name="identity")
-        weight_rows = keep.tile([P, P], F32, name="weight_rows")
+        weight_rows = keep.tile([P, P], F32, name="weight_rows", tag="rows_then_window")
         token_weight = keep.tile([P, S], F32, name="token_weight")
         token_pairs = keep.tile([P, 2 * S], BF16, name="token_pairs")
         planes = [keep.tile([P, T], F32, name=f"plane{n}") for n in range(PLANES)]
@@ -54,7 +54,7 @@ def tile_list_hboth_bias_kernel(tc, xT, w_words, w_scales, wgt, b, wgo, offs, of
         late_words = keep.tile([P, PASSES, 2 * P * (M_TILES - CHUNK_TILES)], U8, name="late_words", align_bytes=64)
         scales = keep.tile([P, PASSES, M], U8, name="scales", align_bytes=64)
         factor = keep.tile([P, S], F32, name="factor")
-        windows = [keep.tile([P, T], F32, name=f"window{n}") for n in range(WINDOWS)]
+        windows = [keep.tile([P, T], F32, name=f"window{n}") for n in range(WINDOWS - 1)]
         bias = keep.tile([P, M_TILES], F32, name="bias")
         chunk_weight = keep.tile([P, CHUNK], F32, name="chunk_weight", tag="held", align_bytes=64)
         codes = {a: keep.tile([P, S], U32, name=f"codes{a}", align_bytes=64) for a in (0, 2)}
@@ -99,6 +99,8 @@ def tile_list_hboth_bias_kernel(tc, xT, w_words, w_scales, wgt, b, wgo, offs, of
 
         turned_rows = turns.tile([P, P], F32, name="turned_rows", tag="turn2")
         nc.tensor.transpose(turned_rows[:], weight_rows[:], identity[:])
+        windows.append(keep.tile([P, T], F32, name="last_window", tag="rows_then_window"))
+        nc.gpsimd.memset(windows[-1][:].bitcast(I32), 0)
         for h in range(2):
             nc.scalar.copy(
                 token_weight[:, HALF * h : HALF * (h + 1)].rearrange("j (n r) -> j n r", r=GROUP),

@@ -72,12 +72,14 @@ def tile_list_hboth_bias_kernel(tc, xT, w_words, w_scales, wgt, b, wgo, offs, of
         first_bias = second_words[:, 0:CHUNK_TILES]
 
         x_view = xT.rearrange("(a p i) t -> a i p t", p=P, i=PACK)
-        nc.sync.dma_start(weight_rows[:], wgt.rearrange("(g r) (c j) -> (r c) g j", g=GROUPS, c=BLOCKS)[0:GROUP])
+        pieces = wgt.rearrange("p (c j) -> (p c) j", j=P)
+        nc.sync.dma_start(weight_rows[0:64, :], pieces[35 : 35 + 7 * 63 + 1 : 7, :])
         nc.sync.dma_start(planes[0][:], x_view[0, 0])
         nc.sync.dma_start(gather_list[:], offs)
         for n in range(1, PLANES):
             nc.sync.dma_start(planes[n][:], x_view[n // PACK, n % PACK])
         make_identity(nc, identity[:])
+        nc.vector.memset(weight_rows[64:P, :], 0.0)
         for window in windows:
             nc.vector.memset(window[:].bitcast(I32), 0)
         nc.vector.memset(scales[:].rearrange("p a n -> p (a n)").bitcast(I32), 0)
@@ -102,15 +104,17 @@ def tile_list_hboth_bias_kernel(tc, xT, w_words, w_scales, wgt, b, wgo, offs, of
         windows.append(keep.tile([P, T], F32, name="last_window", tag="rows_then_window"))
         nc.gpsimd.memset(windows[-1][:].bitcast(I32), 0)
         for h in range(2):
-            nc.scalar.copy(
-                token_weight[:, HALF * h : HALF * (h + 1)].rearrange("j (n r) -> j n r", r=GROUP),
-                turned_rows[:, GROUP * h : GROUP * (h + 1)].unsqueeze(2).to_broadcast([P, GROUP, GROUP]),
-            )
+            for u, first in enumerate((0, 36)):
+                columns = turned_rows[:, first : first + 32].rearrange("j (g e) -> j e g", e=8)[:, 2 - 2 * h : 4 - 2 * h, :]
+                nc.scalar.copy(
+                    token_weight[:, HALF * (1 - h) : HALF * (2 - h)].rearrange("j (c u g r) -> j u c g r", c=2, u=2, r=GROUP)[:, u],
+                    columns.unsqueeze(3).to_broadcast([P, 2, 4, GROUP]),
+                )
         for h in range(2):
             spread = turns.tile([P, HALF], F32, name="spread", tag=f"turn{1 - h}")
             for c in range(2):
                 c0 = HALF * h + P * c
-                nc.tensor.transpose(spread[:, P * c : P * (c + 1)], token_weight[:, c0 : c0 + P], identity[:])
+                nc.tensor.transpose(spread[:, P * c : P * (c + 1)], token_weight[:, S - P - c0 : S - c0], identity[:])
             nc.scalar.copy(weight[:, HALF * h : HALF * (h + 1)], spread[:])
         for held in (early_chunk_weight, chunk_weight):
             nc.scalar.copy(held[:], weight[:, 0:CHUNK])
@@ -134,6 +138,9 @@ def tile_list_hboth_bias_kernel(tc, xT, w_words, w_scales, wgt, b, wgo, offs, of
             for i in range(PACK):
                 if a == 0 and i < 2:
                     nc.vector.tensor_copy(picked[:, i, :], planes[i][:].indirect(gather_list[:]))
+                elif a == 0 and i == 2:
+                    for c0 in (0, HALF):
+                        gather(picked[:, i, c0 : c0 + HALF], i, c0, c0 + HALF, weight[:, c0 : c0 + HALF])
                 else:
                     gather(picked[:, i, :], a * PACK + i, 0, S, weight[:])
             if a == 0:
@@ -149,7 +156,7 @@ def tile_list_hboth_bias_kernel(tc, xT, w_words, w_scales, wgt, b, wgo, offs, of
                             token_pairs[:, 2 * p0 : 2 * (p0 + GROUP)].rearrange("j (r i) -> j i r", i=2),
                             by_token[c // 2][:, c % 2, :, GROUP * g : GROUP * (g + 1)],
                             COPY,
-                            scale=token_weight[:, p0 : p0 + 1],
+                            scale=token_weight[:, p0 + P * (3 - 2 * c) : p0 + P * (3 - 2 * c) + 1],
                         )
                     nc.tensor.transpose(
                         pair_words[:, P * c : P * (c + 1)], token_pairs[:].bitcast(F32)[:, P * c : P * (c + 1)], identity[:]

@@ -30,12 +30,15 @@ CELL = HALF + CHUNK
 GROUPS = 8
 GROUP = P // GROUPS
 BLOCKS = S // P
+REGION = 64 * 1024
+ROW = 4 * T
 
 
 def tile_list_hboth_bias_kernel(tc, xT, w_words, w_scales, wgt, b, wgo, offs, offs2, out):
     nc = tc.nc
     with (
         tc.tile_pool(name="lists", bufs=1) as lists,
+        tc.tile_pool(name="spread_out", bufs=1) as far,
         tc.tile_pool(name="keep", bufs=1) as keep,
         tc.tile_pool(name="work", bufs=2) as work,
         tc.psum_pool(name="banks", bufs=3) as banks,
@@ -46,15 +49,15 @@ def tile_list_hboth_bias_kernel(tc, xT, w_words, w_scales, wgt, b, wgo, offs, of
 
         weight = keep.tile([P, S], F32, name="weight")
         identity = keep.tile([P, P], F32, name="identity")
-        weight_rows = keep.tile([P, P], F32, name="weight_rows", tag="rows_then_window")
+        weight_rows = far.tile([P, P], F32, name="weight_rows", tag="rows_then_window", offset=2 * REGION + 4 * ROW)
         token_weight = keep.tile([P, S], F32, name="token_weight")
         token_pairs = keep.tile([P, 2 * S], BF16, name="token_pairs")
-        planes = [keep.tile([P, T], F32, name=f"plane{n}") for n in range(PLANES)]
+        planes = [far.tile([P, T], F32, name=f"plane{n}", offset=n % 3 * REGION + n // 3 * ROW) for n in range(PLANES)]
         early_words = keep.tile([P, PASSES, 2 * P * CHUNK_TILES], U8, name="early_words", align_bytes=64)
         late_words = keep.tile([P, PASSES, 2 * P * (M_TILES - CHUNK_TILES)], U8, name="late_words", align_bytes=64)
         scales = keep.tile([P, PASSES, M], U8, name="scales", align_bytes=64)
         factor = keep.tile([P, S], F32, name="factor")
-        windows = [keep.tile([P, T], F32, name=f"window{n}") for n in range(WINDOWS - 1)]
+        windows = [far.tile([P, T], F32, name=f"window{n}", offset=n * REGION + 4 * ROW) for n in range(WINDOWS - 1)]
         bias = keep.tile([P, M_TILES], F32, name="bias")
         chunk_weight = keep.tile([P, CHUNK], F32, name="chunk_weight", tag="held", align_bytes=64)
         codes = {a: keep.tile([P, S], U32, name=f"codes{a}", align_bytes=64) for a in (0, 2)}
@@ -101,7 +104,7 @@ def tile_list_hboth_bias_kernel(tc, xT, w_words, w_scales, wgt, b, wgo, offs, of
 
         turned_rows = turns.tile([P, P], F32, name="turned_rows", tag="turn2")
         nc.tensor.transpose(turned_rows[:], weight_rows[:], identity[:])
-        windows.append(keep.tile([P, T], F32, name="last_window", tag="rows_then_window"))
+        windows.append(far.tile([P, T], F32, name="last_window", tag="rows_then_window", offset=2 * REGION + 4 * ROW))
         nc.gpsimd.memset(windows[-1][:].bitcast(I32), 0)
         for h in range(2):
             for u, first in enumerate((0, 36)):

import concourse.mybir as mybir
from concourse.masks import make_identity

K, M, T, S = 1536, 1024, 1024, 512

FLOPS = 2 * K * M * S

F32 = mybir.dt.float32
BF16 = mybir.dt.bfloat16
I32 = mybir.dt.int32
U32 = mybir.dt.uint32
U16 = mybir.dt.uint16
U8 = mybir.dt.uint8
E4M3X4 = mybir.dt.float8_e4m3fn_x4
E2M1X4 = mybir.dt.float4_e2m1fn_x4
MULT = mybir.AluOpType.mult
IDENTITY = mybir.ActivationFunctionType.Identity
COPY = mybir.ActivationFunctionType.Copy

P = 128
PACK = 4
PASSES = K // (P * PACK)
PLANES = PASSES * PACK
M_TILES = M // P
HALF = S // 2
CHUNK = 128
CHUNK_TILES = 2
WINDOWS = 3
CELL = HALF + CHUNK
GROUPS = 8
GROUP = P // GROUPS
BLOCKS = S // P
REGION = 64 * 1024
ROW = 4 * T


def tile_list_hboth_bias_kernel(tc, xT, w_words, w_scales, wgt, b, wgo, offs, offs2, out):
    nc = tc.nc
    with (
        tc.tile_pool(name="lists", bufs=1) as lists,
        tc.tile_pool(name="spread_out", bufs=1) as far,
        tc.tile_pool(name="keep", bufs=1) as keep,
        tc.tile_pool(name="work", bufs=2) as work,
        tc.psum_pool(name="banks", bufs=3) as banks,
        tc.psum_pool(name="turns", bufs=1) as turns,
    ):
        gather_list = lists.tile([P, S // 16], U16, name="gather_list")
        scatter_list = lists.tile([P, S // 16], U16, name="scatter_list")

        weight = keep.tile([P, S], F32, name="weight")
        identity = keep.tile([P, P], F32, name="identity")
        weight_rows = far.tile([P, P], F32, name="weight_rows", tag="rows_then_window", offset=2 * REGION + 4 * ROW)
        token_weight = keep.tile([P, S], F32, name="token_weight")
        token_pairs = keep.tile([P, 2 * S], BF16, name="token_pairs")
        planes = [far.tile([P, T], F32, name=f"plane{n}", offset=n % 3 * REGION + n // 3 * ROW) for n in range(PLANES)]
        early_words = keep.tile([P, PASSES, 2 * P * CHUNK_TILES], U8, name="early_words", align_bytes=64)
        late_words = keep.tile([P, PASSES, 2 * P * (M_TILES - CHUNK_TILES)], U8, name="late_words", align_bytes=64)
        scales = keep.tile([P, PASSES, M], U8, name="scales", align_bytes=64)
        factor = keep.tile([P, S], F32, name="factor")
        windows = [far.tile([P, T], F32, name=f"window{n}", offset=n * REGION + 4 * ROW) for n in range(WINDOWS - 1)]
        bias = keep.tile([P, M_TILES], F32, name="bias")
        chunk_weight = keep.tile([P, CHUNK], F32, name="chunk_weight", tag="held", align_bytes=64)
        codes = {a: keep.tile([P, S], U32, name=f"codes{a}", align_bytes=64) for a in (0, 2)}
        early_chunk_weight = keep.tile([P, CHUNK], F32, name="early_chunk_weight", tag="early_held", align_bytes=64)
        code_scales = {a: keep.tile([P, S], U8, name=f"code_scales{a}", align_bytes=64) for a in (1, 2)}
        first_grouped = keep.tile([P, PACK * HALF], BF16, name="first_grouped", align_bytes=64)
        split_sums = keep.tile([P, WINDOWS, S], F32, name="split_sums")
        last_picked = keep.tile([P, 9 * CELL], F32, name="last_picked", align_bytes=64)

        early_first = last_picked[:, 0 : 2 * S].rearrange("p (v j) -> p v j", v=2)[:, :, 0:HALF]
        late_first = last_picked[:, 3 * CELL : 9 * CELL].rearrange("p (v j) -> p v j", v=2)[:, :, 0:HALF]
        second_picked = last_picked[:, HALF : HALF + 6 * CELL].rearrange("p (u w j) -> p u w j", u=2, w=3)[:, :, ::2, 0:HALF]
        second_words = last_picked[:, 6 * CELL + CHUNK : 6 * CELL + CHUNK + S]
        second_grouped = second_words.bitcast(BF16)
        first_bias = second_words[:, 0:CHUNK_TILES]

        x_view = xT.rearrange("(a p i) t -> a i p t", p=P, i=PACK)
        pieces = wgt.rearrange("p (c j) -> (p c) j", j=P)
        nc.sync.dma_start(weight_rows[0:64, :], pieces[35 : 35 + 7 * 63 + 1 : 7, :])
        nc.sync.dma_start(planes[0][:], x_view[0, 0])
        nc.sync.dma_start(gather_list[:], offs)
        for n in range(1, PLANES):
            nc.sync.dma_start(planes[n][:], x_view[n // PACK, n % PACK])
        make_identity(nc, identity[:])
        nc.vector.memset(weight_rows[64:P, :], 0.0)
        for window in windows:
            nc.vector.memset(window[:].bitcast(I32), 0)
        nc.vector.memset(scales[:].rearrange("p a n -> p (a n)").bitcast(I32), 0)
        scales_view = w_scales.bitcast(I32)
        for r in range(4):
            nc.sync.dma_start(
                scales[r:P:32, :, :].bitcast(I32),
                scales_view[:, r:16:4, :].rearrange("a q n -> q a n"),
            )
        words_view = w_words.bitcast(I32).rearrange("a p n -> p a n")
        bias_view = b.rearrange("(m p) -> p m", p=P)
        nc.sync.dma_start(early_words[:].bitcast(I32), words_view[:, :, 0 : CHUNK_TILES * P // 2])
        with nc.allow_non_contiguous_dma(reason="one bias value a partition and row tile"):
            nc.sync.dma_start(bias[:], bias_view)
        nc.sync.dma_start(scatter_list[:], offs2)
        for c0 in (0, HALF):
            nc.sync.dma_start(factor[:, c0 : c0 + HALF], wgo[:, c0 : c0 + HALF])
        nc.sync.dma_start(late_words[:].bitcast(I32), words_view[:, :, CHUNK_TILES * P // 2 : M // 2])

        turned_rows = turns.tile([P, P], F32, name="turned_rows", tag="turn2")
        nc.tensor.transpose(turned_rows[:], weight_rows[:], identity[:])
        windows.append(far.tile([P, T], F32, name="last_window", tag="rows_then_window", offset=2 * REGION + 4 * ROW))
        nc.gpsimd.memset(windows[-1][:].bitcast(I32), 0)
        for h in range(2):
            for u, first in enumerate((0, 36)):
                columns = turned_rows[:, first : first + 32].rearrange("j (g e) -> j e g", e=8)[:, 2 - 2 * h : 4 - 2 * h, :]
                nc.scalar.copy(
                    token_weight[:, HALF * (1 - h) : HALF * (2 - h)].rearrange("j (c u g r) -> j u c g r", c=2, u=2, r=GROUP)[:, u],
                    columns.unsqueeze(3).to_broadcast([P, 2, 4, GROUP]),
                )
        for h in range(2):
            spread = turns.tile([P, HALF], F32, name="spread", tag=f"turn{1 - h}")
            for c in range(2):
                c0 = HALF * h + P * c
                nc.tensor.transpose(spread[:, P * c : P * (c + 1)], token_weight[:, S - P - c0 : S - c0], identity[:])
            nc.scalar.copy(weight[:, HALF * h : HALF * (h + 1)], spread[:])
        for held in (early_chunk_weight, chunk_weight):
            nc.scalar.copy(held[:], weight[:, 0:CHUNK])

        def gather(picked, n, c0, c1, factors):
            nc.vector.tensor_tensor(picked, planes[n][:].indirect(gather_list[:, c0 // 16 : c1 // 16]), factors, MULT)

        def interleave_pair(grouped, picked, u):
            nc.scalar.copy(
                grouped.rearrange("p (c j u v) -> p u c v j", j=4, u=2, v=2)[:, u],
                picked.rearrange("p v (c j) -> p c v j", j=4),
            )

        def quantize(a, grouped, c0, c1):
            nc.vector.quantize_mx(out=codes[a][:, c0:c1].bitcast(E4M3X4), scales=code_scales[a][:, c0:c1], in_=grouped)

        last = PASSES - 1
        for a in range(last):
            picked = work.tile([P, PACK, S], F32, name="picked")
            grouped = work.tile([P, S * PACK], BF16, name="grouped", align_bytes=64)
            for i in range(PACK):
                if a == 0 and i < 2:
                    nc.vector.tensor_copy(picked[:, i, :], planes[i][:].indirect(gather_list[:]))
                elif a == 0 and i == 2:
                    for c0 in (0, HALF):
                        gather(picked[:, i, c0 : c0 + HALF], i, c0, c0 + HALF, weight[:, c0 : c0 + HALF])
                else:
                    gather(picked[:, i, :], a * PACK + i, 0, S, weight[:])
            if a == 0:
                by_token = [turns.tile([P, 2, 2, P], F32, name=f"by_token{h}", tag=f"turn{h}") for h in range(2)]
                for i in range(2):
                    for c in range(BLOCKS):
                        nc.tensor.transpose(by_token[c // 2][:, c % 2, i, :], picked[:, i, P * c : P * (c + 1)], identity[:])
                pair_words = turns.tile([P, S], F32, name="pair_words", tag="turn2")
                for c in range(BLOCKS):
                    for g in range(GROUPS):
                        p0 = P * c + GROUP * g
                        nc.scalar.activation(
                            token_pairs[:, 2 * p0 : 2 * (p0 + GROUP)].rearrange("j (r i) -> j i r", i=2),
                            by_token[c // 2][:, c % 2, :, GROUP * g : GROUP * (g + 1)],
                            COPY,
                            scale=token_weight[:, p0 + P * (3 - 2 * c) : p0 + P * (3 - 2 * c) + 1],
                        )
                    nc.tensor.transpose(
                        pair_words[:, P * c : P * (c + 1)], token_pairs[:].bitcast(F32)[:, P * c : P * (c + 1)], identity[:]
                    )
                interleave_pair(grouped[:], picked[:, 2:4, :], 1)
                nc.scalar.copy(grouped[:].bitcast(F32).rearrange("p (j u) -> p u j", u=2)[:, 0, :], pair_words[:])
                opening_grouped = grouped
            else:
                nc.scalar.copy(
                    grouped[:].rearrange("p (c j i) -> p c i j", j=4, i=PACK),
                    picked[:].rearrange("p i (c j) -> p c i j", j=4),
                )

        gather(last_picked[:, 0:CHUNK], PLANES - 4, 0, CHUNK, early_chunk_weight[:])
        gather(last_picked[:, CHUNK:S], PLANES - 4, CHUNK, S, weight[:, CHUNK:S])
        code_scales[0] = keep.tile([P, S], U8, name="code_scales0", tag="early_held", align_bytes=64)
        quantize(0, opening_grouped[:], 0, S)
        gather(early_first[:, 1, :], PLANES - 3, 0, HALF, weight[:, 0:HALF])
        interleave_pair(first_grouped[:], early_first, 0)
        gather(last_picked[:, 3 * CELL : 3 * CELL + S], PLANES - 2, 0, S, weight[:])
        gather(late_first[:, 1, 0:CHUNK], PLANES - 1, 0, CHUNK, chunk_weight[:])
        gather(late_first[:, 1, CHUNK:HALF], PLANES - 1, CHUNK, HALF, weight[:, CHUNK:HALF])
        codes[1] = keep.tile([P, S], U32, name="codes1", tag="held", align_bytes=64)
        quantize(1, grouped[:], 0, S)
        for c0 in range(0, HALF, CHUNK):
            chunk = first_grouped[:, PACK * c0 : PACK * (c0 + CHUNK)]
            interleave_pair(chunk, late_first[:, :, c0 : c0 + CHUNK], 1)
            quantize(last, chunk, c0, c0 + CHUNK)
        nc.scalar.copy(first_bias, bias[:, 0:CHUNK_TILES])
        for u in range(2):
            gather(second_picked[:, u, 1, :], last * PACK + 2 * u + 1, HALF, S, weight[:, HALF:S])

        def products(m, c0, c1, columns, sums):
            if m < CHUNK_TILES:
                words, column = early_words, m
            else:
                words, column = late_words, m - CHUNK_TILES
            bank = banks.tile([P, S], F32, name="bank")
            width = S if c1 - c0 == S else CHUNK
            for a in range(PASSES):
                for c in range(c0, c1, width):
                    nc.tensor.matmul_mx(
                        out=bank[:, c - c0 : c - c0 + width],
                        lhsT=words[:, a, 2 * P * column : 2 * P * (column + 1)].bitcast(E2M1X4),
                        lhsT_scale=scales[:, a, P * m : P * (m + 1)],
                        rhs=codes[a][:, c : c + width].bitcast(E4M3X4),
                        rhs_scale=code_scales[a][:, c : c + width],
                        start=(a == 0 and c == c0),
                        stop=(a == last and c == c1 - width),
                    )
            nc.scalar.activation(sums, bank[:, 0 : c1 - c0], IDENTITY, bias=columns[:, m : m + 1])

        def row_tile(m, c0, c1, columns, sums):
            step = CHUNK if m == 0 else c1 - c0
            for c in range(c0, c1, step):
                products(m, c, c + step, columns, sums[:, c - c0 : c - c0 + step])
            window = windows[m % WINDOWS]
            nc.vector.tensor_tensor(window[:].indirect(scatter_list[:, c0 // 16 : c1 // 16]), sums, factor[:, c0:c1], MULT)
            if c1 == S:
                nc.sync.dma_start(out[P * m : P * (m + 1), :], window[:])

        cuts = (HALF, CHUNK, HALF)
        for m in (1, 0):
            row_tile(m, 0, cuts[m], first_bias, split_sums[:, m, 0 : cuts[m]])
        nc.scalar.copy(
            second_grouped.rearrange("p (c j u v) -> p c u v j", j=4, u=2, v=2),
            second_picked.rearrange("p u v (c j) -> p c u v j", j=4),
        )
        for c0 in range(HALF, S, CHUNK):
            quantize(last, second_grouped[:, PACK * (c0 - HALF) : PACK * (c0 - HALF + CHUNK)], c0, c0 + CHUNK)
        row_tile(WINDOWS - 1, 0, HALF, bias, second_picked[:, 1, 0, :])
        for m in range(WINDOWS):
            row_tile(m, cuts[m], S, bias, split_sums[:, m, cuts[m] : S])
        for m in range(WINDOWS, M_TILES):
            sums = work.tile([P, S], F32, name="sums")
            row_tile(m, 0, S, bias, sums[:])
